import numpy as np
import ml_dtypes


def mxq(x, axis, fmt="e4m3"):
    dtype, down = {"e4m3": (ml_dtypes.float8_e4m3fn, 7), "e5m2": (ml_dtypes.float8_e5m2, 14)}[fmt]
    v = np.moveaxis(np.asarray(x, np.float32).astype(ml_dtypes.bfloat16).astype(np.float64), axis, -1)
    blocks = v.reshape(v.shape[:-1] + (-1, 32))
    amax = np.abs(blocks).max(-1, keepdims=True)
    byte = np.maximum(np.where(amax > 0, np.frexp(amax)[1] - 1 + 127, 0) - down, 1)
    scale = np.exp2(byte - 127.0)
    codes = (blocks / scale).astype(np.float32).astype(dtype).astype(np.float64)
    return np.moveaxis((codes * scale).reshape(v.shape), -1, axis)


WIDE = False


def mx_kscale(k):
    if not WIDE:
        return np.ones(k)
    levels = np.array([10, -10, 5, -5, 0])
    if k % 512:
        return np.exp2(np.random.permutation(np.resize(levels, k // 32))).repeat(32)
    a = np.empty((k // 512, 16))
    for p in range(k // 512):
        a[p, :8] = np.random.permutation(np.resize(levels, 8))
        for g in range(8):
            far = levels[np.abs(levels - a[p, g]) >= 10]
            a[p, g + 8] = far[np.random.randint(len(far))]
    return np.exp2(a.ravel()).repeat(32)


def f64(x):
    return np.asarray(x).astype(np.float64)


def striped(idx):
    return np.tile(idx.reshape(-1, 16).T, (8, 1)).astype(np.uint16)


def unstriped(offs):
    return offs[:16].T.reshape(-1).astype(np.int64)


E2M1 = np.array([0.0, 0.5, 1.0, 1.5, 2.0, 3.0, 4.0, 6.0, -0.0, -0.5, -1.0, -1.5, -2.0, -3.0, -4.0, -6.0])


def pack_weight(w, fmt):
    k, n = w.shape
    w = f64(np.asarray(w, np.float32).astype(ml_dtypes.bfloat16)).reshape(k // 32, 32, n)
    amax = np.abs(w).max(1)
    if fmt == "e4m3":
        byte = np.frexp(amax)[1] - 1 + 127 - 7
    else:
        mant, ex = np.frexp(amax / 6.0)
        byte = np.where(mant > 0.5, ex, ex - 1) + 127
    byte = np.clip(np.where(amax > 0, byte, 1), 1, 254)
    scaled = (w * np.exp2(127.0 - byte)[:, None, :]).reshape(k, n).astype(np.float32)
    by_word = np.ascontiguousarray(scaled.reshape(k // 512, 128, 4, n).transpose(0, 1, 3, 2))
    if fmt == "e4m3":
        words = by_word.astype(ml_dtypes.float8_e4m3fn).view(np.uint8)
    else:
        c = by_word.astype(ml_dtypes.float4_e2m1fn).view(np.uint8) & 0xF
        words = (c[..., 0::2] | (c[..., 1::2] << 4)).reshape(k // 512, 128, 2 * n)
    return np.ascontiguousarray(words), np.ascontiguousarray(byte.astype(np.uint8).reshape(k // 512, 16, n))


def unpack_weight(words, scales, fmt):
    g, _, n = scales.shape
    words = np.ascontiguousarray(words).reshape(g, 128, n, -1)
    if fmt == "e4m3":
        vals = words.view(ml_dtypes.float8_e4m3fn).astype(np.float64)
    else:
        nib = np.empty((g, 128, n, 4), np.uint8)
        nib[..., 0::2] = words & 0xF
        nib[..., 1::2] = words >> 4
        vals = E2M1[nib]
    vals = vals * np.repeat(np.exp2(scales.astype(np.float64) - 127.0), 8, axis=1)[..., None]
    return vals.transpose(0, 1, 3, 2).reshape(g * 512, n)


def gelu(v):
    return 0.5 * v * (1.0 + np.tanh(np.sqrt(2.0 / np.pi) * (v + 0.044715 * v**3)))


def bf(x):
    return np.asarray(x, np.float32).astype(ml_dtypes.bfloat16)


def planes(Y):
    n, m = Y.shape
    b = f64(bf(Y)).reshape(n // 32, 32, m)
    amax = np.abs(b).max(1)
    byte = np.clip(np.where(amax > 0, np.frexp(amax)[1] - 1 + 127 - 7, 1), 1, 254)
    codes = (b * np.exp2(127.0 - byte)[:, None, :]).reshape(n, m).astype(np.float32).astype(ml_dtypes.float8_e4m3fn).view(np.uint8)
    words = codes.reshape(n // 512, 128, 4, m).transpose(0, 1, 3, 2)
    return np.ascontiguousarray(words), np.ascontiguousarray(byte.astype(np.uint8).reshape(n // 512, 16, m))


K, M, H, T, S, T2, P = 1024, 512, 512, 4096, 1024, 2048, 1024

def setup_inputs():
    n = np.random.standard_normal
    s, um, u = mx_kscale(K)[:, None], mx_kscale(M)[:, None], mx_kscale(H)[:, None]
    eg = np.exp(0.8 * n(H))
    d = {}
    d["tab_words"], d["tab_scales"] = pack_weight(n((K, T)) * s, "e4m3")
    d["offs"] = striped(np.random.permutation(T)[:S])
    d["w1"] = (1.3 * n((K, M)) / K ** 0.5 / s).astype(np.float32)
    d["gm"] = (0.5 * np.exp(0.3 * n(M)) * um[:, 0]).astype(np.float32)
    d["w2_words"], d["w2_scales"] = pack_weight(n((M, H)) / M ** 0.5 / um * u.T, "e4m3")
    d["w3_words"], d["w3_scales"] = pack_weight(n((K, H)) / K ** 0.5 / s * u.T, "e2m1")
    d["wgs"] = np.exp(np.random.uniform(-0.3, 0.3, (128, S))).astype(np.float32)
    d["page0"] = (np.random.uniform(-4.5, 4.5, (H, T2)) * u).astype(np.float32)
    d["offs2"] = striped(np.random.permutation(T2)[:S])
    d["offs3"] = striped(np.random.permutation(T2)[:P])
    d["gs"] = (np.random.uniform(0.28, 0.46, H) / u[:, 0]).astype(np.float32)
    d["gx"] = (np.exp(0.4 * n(H)) * u[:, 0]).astype(np.float32)
    d["w4"] = (n((H, H)) / H ** 0.5 / u * eg[None, :]).astype(np.float32)
    d["offs4"] = striped(np.random.permutation(T2)[:P])
    d["gg"] = (np.random.uniform(0.25, 0.5, H) * eg / u[:, 0]).astype(np.float32)
    return d

def reference(tab_words, tab_scales, offs, w1, gm, w2_words, w2_scales, w3_words, w3_scales, wgs, page0, offs2, offs3, gs, gx, w4, offs4, gg):
    v = unpack_weight(tab_words, tab_scales, "e4m3")[:, unstriped(offs)]
    w2 = unpack_weight(w2_words, w2_scales, "e4m3")
    w3 = unpack_weight(w3_words, w3_scales, "e2m1")
    b = mxq(f64(w1), 0, "e4m3").T @ v
    a = f64(gm)[:, None] * b * (1.0 + np.tanh(0.7978845608 * (b + 0.044715 * b ** 3)))
    h = np.minimum(w2.T @ mxq(a, 0, "e4m3"), w3.T @ v)
    page = f64(page0).copy()
    page[:, unstriped(offs2)] = np.tile(f64(wgs), (H // 128, 1)) * h
    x = page[:, unstriped(offs3)]
    x = f64(gx)[:, None] * np.sin(f64(gs)[:, None] * x)
    golden = page[:, unstriped(offs4)]
    y = (mxq(f64(w4), 0, "e4m3").T @ mxq(x, 0, "e4m3")) - f64(gg)[:, None] * golden
    words, scales = planes(y)
    return y, words, scales

@@ -1,0 +1,416 @@
+from contextlib import ExitStack
+
+import concourse.mybir as mybir
+
+K, M, H, T, S, T2, NP = 1024, 512, 512, 4096, 1024, 2048, 1024
+FLOPS = 2 * (K * M * S + M * H * S + K * H * S + H * H * NP)
+
+F32 = mybir.dt.float32
+BF16 = mybir.dt.bfloat16
+I32 = mybir.dt.int32
+U32 = mybir.dt.uint32
+U16 = mybir.dt.uint16
+U8 = mybir.dt.uint8
+FP8X4 = mybir.dt.float8_e4m3fn_x4
+FP4X4 = mybir.dt.float4_e2m1fn_x4
+ALU = mybir.AluOpType
+ACT = mybir.ActivationFunctionType
+
+P = 128
+PACK = 4
+HALF = 512
+CHUNK = 256
+LIST_ROWS = 16
+KB = 1024
+
+
+def list_slice(offsets, first, count):
+    return offsets[:, first // LIST_ROWS : (first + count) // LIST_ROWS]
+
+
+def weave_out(tile):
+    return tile.rearrange("p (c i) t -> p c t i", i=4)
+
+
+def weave_in(tile):
+    return tile.rearrange("p t (c i) -> p c t i", i=4)
+
+
+def tile_list_panel_node_features_kernel(
+    tc, tab_words, tab_scales, offs, w1, gm, w2_words, w2_scales, w3_words, w3_scales,
+    wgs, page0, offs2, offs3, gs, gx, w4, offs4, gg, out_0, out_1, out_2,
+):
+    nc = tc.nc
+    with ExitStack() as ctx:
+        keep = ctx.enter_context(tc.tile_pool(name="keep", bufs=1))
+        slide = ctx.enter_context(tc.tile_pool(name="slide", bufs=1))
+        ring = ctx.enter_context(tc.tile_pool(name="ring", bufs=2))
+        psum = ctx.enter_context(tc.psum_pool(name="psum", bufs=1))
+
+        def held(shape, dtype, name, tag=None):
+            return keep.tile(shape, dtype, name=name, tag=tag or name, align_bytes=64)
+
+        def bank(tag, bufs, name):
+            return psum.tile([P, HALF], F32, name=name, tag=tag, bufs=bufs)
+
+        lists = {}
+        for name in ("offs", "offs2", "offs3", "offs4"):
+            lists[name] = held([P, S // LIST_ROWS], U16, "list_" + name)
+
+        tab_s = held([P, T], U8, "tab_s")
+        wsc_raw = held([P, 3, H], U8, "wsc_raw")
+        v_scale1 = held([P, S], U8, "v_scale1")
+        warm = held([P, 1], F32, "warm")
+        nc.vector.memset(tab_s[:].bitcast(I32), 0)
+        nc.vector.memset(warm[:], 0.0)
+        nc.gpsimd.memset(wsc_raw[:].rearrange("p a c -> p (a c)").bitcast(I32), 0)
+        nc.vector.memset(v_scale1[:].bitcast(I32), 0)
+
+        nc.sync.dma_start(lists["offs"][:], offs)
+        for q in range(4):
+            nc.scalar.dma_start(
+                tab_s[32 * q : 32 * q + 8, :].bitcast(I32),
+                tab_scales[:, 4 * q : 4 * q + 4, :].bitcast(I32),
+            )
+        warm_out = held([P, 1], F32, "warm_out")
+        nc.scalar.activation(warm_out[:], warm[:], ACT.Gelu_apprx_tanh)
+        gm_col = held([P, PACK], F32, "gm_col")
+        gg_col = held([P, PACK], F32, "gg_col")
+        for tile, vec in ((gm_col, gm), (gg_col, gg)):
+            nc.gpsimd.dma_start(tile[:], vec.rearrange("(p t) -> p t", t=PACK))
+        gm2 = held([P, PACK], F32, "gm2")
+        nc.scalar.activation(gm2[:], gm_col[:], ACT.Copy, scale=2.0)
+        gg_neg = held([P, PACK], F32, "gg_neg")
+        nc.scalar.activation(gg_neg[:], gg_col[:], ACT.Copy, scale=-1.0)
+        w3_raw = held([P, 2, 2 * H], U8, "w3_raw")
+        nc.sync.dma_start(w3_raw[:].bitcast(I32), w3_words.rearrange("a p b -> p a b").bitcast(I32))
+        for q in range(4):
+            nc.gpsimd.dma_start(
+                wsc_raw[32 * q : 32 * q + 4, 0:2, :].bitcast(I32),
+                w3_scales[:, 4 * q : 4 * q + 4, :].rearrange("a r c -> r a c").bitcast(I32),
+            )
+        for q in range(4):
+            nc.gpsimd.dma_start(
+                wsc_raw[32 * q : 32 * q + 4, 2, :].bitcast(I32),
+                w2_scales[0, 4 * q : 4 * q + 4, :].bitcast(I32),
+            )
+        gs_col = held([P, PACK], F32, "gs_col")
+        gx_col = held([P, PACK], F32, "gx_col")
+        for tile, vec in ((gs_col, gs), (gx_col, gx)):
+            nc.gpsimd.dma_start(tile[:], vec.rearrange("(p t) -> p t", t=PACK))
+        tab_rows = tab_words.rearrange("a p t i -> a p (t i)").bitcast(I32)
+        w1_rows = w1.rearrange("(a p j) m -> a p j m", a=2, j=PACK)
+        tab_w = []
+        w1_raw = []
+        tab_w.append(held([P, T], I32, "tab_w0"))
+        nc.sync.dma_start(tab_w[0][:], tab_rows[0])
+        for u in range(2):
+            tile = held([P, PACK, M // 2], F32, "w1_raw0%d" % u)
+            nc.sync.dma_start(tile[:], w1_rows[0][:, :, u * 256 : (u + 1) * 256])
+            w1_raw.append(tile)
+        tab_w.append(held([P, T], I32, "tab_w1"))
+        nc.sync.dma_start(tab_w[1][:], tab_rows[1])
+        for u in range(2):
+            tile = held([P, PACK, M // 2], F32, "w1_raw1%d" % u)
+            nc.sync.dma_start(tile[:], w1_rows[1][:, :, u * 256 : (u + 1) * 256])
+            w1_raw.append(tile)
+
+        picked_s = held([P, S], U8, "picked_s")
+        nc.vector.tensor_copy(picked_s[:], tab_s[:].indirect(lists["offs"][:]))
+        nc.scalar.dma_start(v_scale1[0:124, :].bitcast(I32), picked_s[4:128, :].bitcast(I32))
+        v_plane = [picked_s, v_scale1]
+
+        w3_c = held([P, 2, 2 * H], U8, "w3_c")
+        nc.vector.tensor_copy(
+            w3_c[:].bitcast(U16).rearrange("p a (t q) -> p a q t", t=PACK),
+            w3_raw[:].bitcast(U16).rearrange("p a (q t) -> p a q t", t=PACK),
+        )
+
+        v_words = [[None, None], [None, None]]
+
+        def pick_table(a, u):
+            tile = held([P, HALF], I32, "v_words%d%d" % (a, u))
+            nc.vector.tensor_copy(
+                tile[:].bitcast(U32),
+                tab_w[a][:].bitcast(U32).indirect(list_slice(lists["offs"], u * HALF, HALF)),
+            )
+            v_words[a][u] = tile
+
+        pick_table(0, 0)
+        pick_table(1, 0)
+
+        w1_c = held([P, 2, M], U32, "w1_c")
+        w1_s = held([P, 2, M], U8, "w1_s")
+        w1_b = [held([P, PACK, P, PACK], BF16, "w1_b%d" % a) for a in range(2)]
+        for a in range(2):
+            for u in range(2):
+                copy = nc.vector.tensor_copy if (a, u) in ((1, 1),) else nc.scalar.copy
+                copy(
+                    w1_b[a][:, :, 64 * u : 64 * (u + 1), :].rearrange("p t q j -> p q j t"),
+                    w1_raw[2 * a + u][:].rearrange("p j (q t) -> p q j t", t=PACK),
+                )
+            nc.vector.quantize_mx(
+                out=w1_c[:, a, :].bitcast(FP8X4), scales=w1_s[:, a, :],
+                in_=w1_b[a][:].rearrange("p t q j -> p (t q j)"),
+            )
+        w3_s = held([P, 2, H], U8, "w3_s")
+        nc.vector.tensor_copy(
+            w3_s[:].rearrange("p a (t q) -> p a q t", t=PACK),
+            wsc_raw[:, 0:2, :].rearrange("p a (q t) -> p a q t", t=PACK),
+        )
+
+        h3 = held([P, PACK, S], F32, "h3", tag="h3")
+
+        def second_reading(first):
+            u, c0 = divmod(first, HALF)
+            for pair in range(2):
+                acc = bank("pa", 2, "acc3")
+                for s in range(2):
+                    t = 2 * pair + s
+                    for n0 in range(0, CHUNK, P):
+                        for a in range(2):
+                            nc.tensor.matmul_mx(
+                                out=acc[:, s * CHUNK + n0 : s * CHUNK + n0 + P],
+                                lhsT=w3_c[:, a, t * 256 : (t + 1) * 256].bitcast(FP4X4),
+                                lhsT_scale=w3_s[:, a, t * P : (t + 1) * P],
+                                rhs=v_words[a][u][:, c0 + n0 : c0 + n0 + P].bitcast(FP8X4),
+                                rhs_scale=v_plane[a][:, first + n0 : first + n0 + P],
+                                start=(a == 0), stop=(a == 1),
+                            )
+                nc.scalar.copy(
+                    h3[:, 2 * pair : 2 * pair + 2, first : first + CHUNK],
+                    acc[:].rearrange("p (s n) -> p s n", s=2),
+                )
+
+        w2_raw = held([P, H], I32, "w2_raw")
+        nc.sync.dma_start(w2_raw[:], w2_words[0].rearrange("p c i -> p (c i)").bitcast(I32))
+        page_rows = page0.rearrange("(p t) c -> t p c", t=PACK)
+        wgs_rows = wgs.rearrange("(q t) j -> q t j", t=PACK)
+        page = [
+            held([P, T2], F32, "page%d" % t) for t in range(PACK)
+        ]
+        gain = {
+            0: held([P, PACK, CHUNK], F32, "gain0"),
+            CHUNK: held([P, PACK, CHUNK], F32, "gain1"),
+            HALF: held([P, PACK, HALF], F32, "gain2"),
+        }
+
+        def load_gain(first, count):
+            for q in (0, 2, 1, 3):
+                nc.sync.dma_start(
+                    gain[first][32 * q : 32 * q + 32, :, :], wgs_rows[:, :, first : first + count]
+                )
+
+        nc.sync.dma_start(page[0][:], page_rows[0])
+        nc.sync.dma_start(lists["offs2"][:], offs2)
+        load_gain(0, CHUNK)
+        nc.sync.dma_start(page[1][:], page_rows[1])
+        load_gain(CHUNK, CHUNK)
+        nc.sync.dma_start(page[2][:], page_rows[2])
+        nc.sync.dma_start(page[3][:], page_rows[3])
+        load_gain(HALF, HALF)
+        nc.sync.dma_start(lists["offs3"][:], offs3)
+        nc.sync.dma_start(lists["offs4"][:], offs4)
+        w4_raw = held([P, PACK, H], F32, "w4_raw")
+        nc.sync.dma_start(w4_raw[:], w4.rearrange("(p j) n -> p j n", j=PACK))
+
+        w2_c = held([P, H], I32, "w2_c")
+        w2_s = held([P, H], U8, "w2_s")
+        nc.vector.tensor_copy(
+            w2_c[:].rearrange("p (t q) -> p q t", t=PACK),
+            w2_raw[:].rearrange("p (q t) -> p q t", t=PACK),
+        )
+        nc.vector.tensor_copy(
+            w2_s[:].rearrange("p (t q) -> p q t", t=PACK),
+            wsc_raw[:, 2, :].rearrange("p (q t) -> p q t", t=PACK),
+        )
+
+        a_s = held([P, S], U8, "a_s")
+        h = {}
+
+        def scatter(first, tiles):
+            start = min(first, HALF)
+            for t in tiles:
+                nc.vector.tensor_tensor(
+                    page[t][:].indirect(list_slice(lists["offs2"], first, CHUNK)),
+                    h[first, t // 2][:, t % 2, :],
+                    gain[start][:, t, first - start : first - start + CHUNK],
+                    ALU.mult,
+                )
+
+        for c in range(S // CHUNK):
+            first = c * CHUNK
+            u, c0 = divmod(first, HALF)
+            cols = slice(first, first + CHUNK)
+            gel = ring.tile([P, PACK, CHUNK], F32, name="gel", tag="gel", align_bytes=64)
+            for pair in range(2):
+                acc = bank("pb", 3, "acc1")
+                for s in range(2):
+                    t = 2 * pair + s
+                    for a in range(2):
+                        nc.tensor.matmul_mx(
+                            out=acc[:, s * CHUNK : (s + 1) * CHUNK],
+                            lhsT=w1_c[:, a, t * P : (t + 1) * P].bitcast(FP8X4),
+                            lhsT_scale=w1_s[:, a, t * P : (t + 1) * P],
+                            rhs=v_words[a][u][:, c0 : c0 + CHUNK].bitcast(FP8X4),
+                            rhs_scale=picked_s[4 * a : P, cols],
+                            start=(a == 0), stop=(a == 1),
+                        )
+                nc.scalar.activation(
+                    gel[:, 2 * pair : 2 * pair + 2, :].rearrange("p s n -> p (s n)"),
+                    acc[:], ACT.Gelu_apprx_tanh,
+                )
+            second_reading(first)
+            if c == 0:
+                pick_table(0, 1)
+                pick_table(1, 1)
+            a_b = ring.tile([P, CHUNK, PACK], BF16, name="a_b", align_bytes=64)
+            if c == 0:
+                nc.vector.tensor_tensor(
+                    weave_out(a_b[:]), weave_in(gel[:]),
+                    gm2[:].unsqueeze(1).unsqueeze(3).to_broadcast([P, CHUNK // 4, PACK, 4]),
+                    ALU.mult,
+                )
+            else:
+                a_rows = held([P, PACK, CHUNK], BF16, "a_rows")
+                for t in range(PACK):
+                    nc.scalar.activation(
+                        a_rows[:, t, :], gel[:, t, :], ACT.Copy, scale=gm2[:, t : t + 1]
+                    )
+                nc.scalar.copy(weave_out(a_b[:]), weave_in(a_rows[:]))
+            if c == 0:
+                a_c = held([P, CHUNK], U32, "a_c")
+            else:
+                a_c = slide.tile([P, CHUNK], U32, name="a_c%d" % c, offset=(c - 1) * KB, align_bytes=64)
+            nc.vector.quantize_mx(
+                out=a_c[:].bitcast(FP8X4), scales=a_s[:, cols],
+                in_=a_b[:].rearrange("p n t -> p (n t)"),
+            )
+            for pair in range(2):
+                acc = bank("pc", 3, "acc2")
+                for s in range(2):
+                    t = 2 * pair + s
+                    nc.tensor.matmul_mx(
+                        out=acc[:, s * CHUNK : (s + 1) * CHUNK],
+                        lhsT=w2_c[:, t * P : (t + 1) * P].bitcast(FP8X4),
+                        lhsT_scale=w2_s[:, t * P : (t + 1) * P],
+                        rhs=a_c[:].bitcast(FP8X4),
+                        rhs_scale=a_s[:, cols],
+                        start=True, stop=True,
+                    )
+                tile = slide.tile(
+                    [P, 2, CHUNK], F32, name="h%d%d" % (c, pair), offset=(c + 2 * pair) * KB,
+                    align_bytes=64,
+                )
+                h[first, pair] = tile
+                nc.vector.tensor_tensor(
+                    tile[:],
+                    acc[:].rearrange("p (s n) -> p s n", s=2),
+                    h3[:, 2 * pair : 2 * pair + 2, cols],
+                    ALU.min,
+                )
+            if c < S // CHUNK - 1:
+                scatter(first, range(PACK))
+
+        w4_b = held([P, PACK, P, PACK], BF16, "w4_b", tag="a_rows")
+        nc.scalar.copy(
+            w4_b[:].rearrange("p t q j -> p q j t"),
+            w4_raw[:].rearrange("p j (q t) -> p q j t", t=PACK),
+        )
+        w4_c = held([P, H], U32, "w4_c")
+        w4_s = held([P, H], U8, "w4_s")
+        nc.vector.quantize_mx(
+            out=w4_c[:].bitcast(FP8X4), scales=w4_s[:],
+            in_=w4_b[:].rearrange("p t q j -> p (t q j)"),
+        )
+
+        x_rows = [held([P, PACK, HALF], BF16, "x_rows%d" % u, tag="w1_raw0%d" % u) for u in range(2)]
+
+        def reread(t):
+            pieces = 2 if t == PACK - 1 else 1
+            width = NP // pieces
+            picked = held([P, NP], F32, "picked%d" % t)
+            for piece in range(pieces):
+                cols = slice(piece * width, (piece + 1) * width)
+                nc.vector.tensor_copy(
+                    picked[:, cols],
+                    page[t][:].indirect(list_slice(lists["offs3"], piece * width, width)),
+                )
+                sine = ring.tile([P, width], F32, name="sine", tag="gel", align_bytes=64)
+                nc.scalar.activation(sine[:], picked[:, cols], ACT.Sin, scale=gs_col[:, t : t + 1])
+                for u in range(2) if pieces == 1 else [piece]:
+                    c0 = u * HALF - piece * width
+                    nc.scalar.activation(
+                        x_rows[u][:, t, :], sine[:, c0 : c0 + HALF], ACT.Copy,
+                        scale=gx_col[:, t : t + 1],
+                    )
+
+        for t in range(PACK):
+            scatter(S - CHUNK, [t])
+            if t > 0:
+                reread(t - 1)
+        reread(PACK - 1)
+
+        x_c = held([P, NP], U32, "x_c")
+        x_s = held([P, NP], U8, "x_s")
+        y = held([P, PACK, NP], F32, "y", tag="h3")
+        y_c = held([P, NP], I32, "y_c")
+        y_s = held([P, NP], U8, "y_s")
+        out_rows = out_0.rearrange("(p t) j -> t p j", t=PACK)
+        out_words = out_1[0].rearrange("p m t -> p (m t)").bitcast(I32)
+        for u in range(2):
+            cols = slice(u * HALF, (u + 1) * HALF)
+            x_b = held([P, HALF, PACK], BF16, "x_b%d" % u, tag="w1_raw1%d" % u)
+            nc.scalar.copy(weave_out(x_b[:]), weave_in(x_rows[u][:]))
+            if u == 0:
+                whole = held([P, PACK, HALF], F32, "golden0", tag="gain2")
+                golden = [whole[:, t, :] for t in range(PACK)]
+            else:
+                early = held([P, 2, HALF], F32, "golden1a")
+                late = held([P, 1, HALF], F32, "golden1b", tag="w1_raw10")
+                last = held([P, HALF], F32, "golden1c", tag="w1_raw11")
+                golden = [early[:, t, :] for t in range(2)] + [late[:, t, :] for t in range(1)] + [last[:]]
+            nc.vector.quantize_mx(
+                out=x_c[:, cols].bitcast(FP8X4), scales=x_s[:, cols],
+                in_=x_b[:].rearrange("p n t -> p (n t)"),
+            )
+            for t in range(PACK):
+                nc.vector.tensor_copy(
+                    golden[t],
+                    page[t][:].indirect(list_slice(lists["offs4"], u * HALF, HALF)),
+                )
+            for t in range(PACK):
+                acc = bank("pa", 2, "acc4") if t % 2 == 0 else bank("pb", 3, "acc4")
+                nc.tensor.matmul_mx(
+                    out=acc[:],
+                    lhsT=w4_c[:, t * P : (t + 1) * P].bitcast(FP8X4),
+                    lhsT_scale=w4_s[:, t * P : (t + 1) * P],
+                    rhs=x_c[:, cols].bitcast(FP8X4),
+                    rhs_scale=x_s[:, cols],
+                    start=True, stop=True,
+                )
+                nc.vector.scalar_tensor_tensor(
+                    y[:, t, cols], golden[t], gg_neg[:, t : t + 1], acc[:],
+                    ALU.mult, ALU.add,
+                )
+                nc.sync.dma_start(out_rows[t][:, cols], y[:, t, cols])
+            y_b = held([P, HALF, PACK], BF16, "y_b%d" % u, tag="w1_b%d" % u)
+            if u == 0:
+                nc.scalar.copy(weave_out(y_b[:]), weave_in(y[:, :, cols]))
+            else:
+                nc.scalar.copy(
+                    weave_out(y_b[:, 0:CHUNK, :]), weave_in(y[:, :, HALF : HALF + CHUNK])
+                )
+                nc.vector.tensor_copy(
+                    weave_out(y_b[:, CHUNK:HALF, :]), weave_in(y[:, :, HALF + CHUNK : NP])
+                )
+            nc.vector.quantize_mx(
+                out=y_c[:, cols].bitcast(FP8X4), scales=y_s[:, cols],
+                in_=y_b[:].rearrange("p n t -> p (n t)"),
+            )
+            nc.sync.dma_start(out_words[:, cols], y_c[:, cols])
+        for q in range(4):
+            (nc.scalar if q % 2 == 0 else nc.sync).dma_start(
+                out_2[0, 4 * q : 4 * q + 4, :].bitcast(I32),
+                y_s[32 * q : 32 * q + 4, :].bitcast(I32),
+            )

@@ -59,66 +59,51 @@ def tile_list_panel_node_features_kernel(
 
         tab_s = held([P, T], U8, "tab_s")
         wsc_raw = held([P, 3, H], U8, "wsc_raw")
-        v_scale1 = held([P, S], U8, "v_scale1")
+        v_scale = held([P, 2, S], U8, "v_scale")
         warm = held([P, 1], F32, "warm")
-        nc.vector.memset(tab_s[:].bitcast(I32), 0)
-        nc.vector.memset(warm[:], 0.0)
-        nc.gpsimd.memset(wsc_raw[:].rearrange("p a c -> p (a c)").bitcast(I32), 0)
-        nc.vector.memset(v_scale1[:].bitcast(I32), 0)
+        nc.vector.memset(wsc_raw[:].rearrange("p a c -> p (a c)").bitcast(I32), 0)
+        nc.vector.memset(tab_s[32:64, :].bitcast(I32), 0)
+        nc.vector.memset(tab_s[64:128, :].bitcast(I32), 0)
+        nc.vector.memset(v_scale[:].rearrange("p a c -> p (a c)").bitcast(I32), 0)
 
+        nc.sync.dma_start(
+            tab_s[0:32, :].bitcast(I32), tab_scales.rearrange("a q t -> (a q) t").bitcast(I32)
+        )
         nc.sync.dma_start(lists["offs"][:], offs)
-        for q in range(4):
-            nc.scalar.dma_start(
-                tab_s[32 * q : 32 * q + 8, :].bitcast(I32),
-                tab_scales[:, 4 * q : 4 * q + 4, :].bitcast(I32),
-            )
-        warm_out = held([P, 1], F32, "warm_out")
-        nc.scalar.activation(warm_out[:], warm[:], ACT.Gelu_apprx_tanh)
-        gm_col = held([P, PACK], F32, "gm_col")
-        gg_col = held([P, PACK], F32, "gg_col")
-        for tile, vec in ((gm_col, gm), (gg_col, gg)):
-            nc.gpsimd.dma_start(tile[:], vec.rearrange("(p t) -> p t", t=PACK))
-        gm2 = held([P, PACK], F32, "gm2")
-        nc.scalar.activation(gm2[:], gm_col[:], ACT.Copy, scale=2.0)
-        gg_neg = held([P, PACK], F32, "gg_neg")
-        nc.scalar.activation(gg_neg[:], gg_col[:], ACT.Copy, scale=-1.0)
         w3_raw = held([P, 2, 2 * H], U8, "w3_raw")
         nc.sync.dma_start(w3_raw[:].bitcast(I32), w3_words.rearrange("a p b -> p a b").bitcast(I32))
         for q in range(4):
-            nc.gpsimd.dma_start(
+            nc.scalar.dma_start(
                 wsc_raw[32 * q : 32 * q + 4, 0:2, :].bitcast(I32),
                 w3_scales[:, 4 * q : 4 * q + 4, :].rearrange("a r c -> r a c").bitcast(I32),
             )
-        for q in range(4):
-            nc.gpsimd.dma_start(
-                wsc_raw[32 * q : 32 * q + 4, 2, :].bitcast(I32),
-                w2_scales[0, 4 * q : 4 * q + 4, :].bitcast(I32),
-            )
-        gs_col = held([P, PACK], F32, "gs_col")
-        gx_col = held([P, PACK], F32, "gx_col")
-        for tile, vec in ((gs_col, gs), (gx_col, gx)):
-            nc.gpsimd.dma_start(tile[:], vec.rearrange("(p t) -> p t", t=PACK))
+        nc.vector.memset(warm[:], 0.0)
+        warm_out = held([P, 1], F32, "warm_out")
+        nc.scalar.activation(warm_out[:], warm[:], ACT.Gelu_apprx_tanh)
         tab_rows = tab_words.rearrange("a p t i -> a p (t i)").bitcast(I32)
         w1_rows = w1.rearrange("(a p j) m -> a p j m", a=2, j=PACK)
-        tab_w = []
-        w1_raw = []
-        tab_w.append(held([P, T], I32, "tab_w0"))
-        nc.sync.dma_start(tab_w[0][:], tab_rows[0])
-        for u in range(2):
-            tile = held([P, PACK, M // 2], F32, "w1_raw0%d" % u)
-            nc.sync.dma_start(tile[:], w1_rows[0][:, :, u * 256 : (u + 1) * 256])
-            w1_raw.append(tile)
-        tab_w.append(held([P, T], I32, "tab_w1"))
-        nc.sync.dma_start(tab_w[1][:], tab_rows[1])
-        for u in range(2):
-            tile = held([P, PACK, M // 2], F32, "w1_raw1%d" % u)
-            nc.sync.dma_start(tile[:], w1_rows[1][:, :, u * 256 : (u + 1) * 256])
-            w1_raw.append(tile)
-
         picked_s = held([P, S], U8, "picked_s")
         nc.vector.tensor_copy(picked_s[:], tab_s[:].indirect(lists["offs"][:]))
-        nc.scalar.dma_start(v_scale1[0:124, :].bitcast(I32), picked_s[4:128, :].bitcast(I32))
-        v_plane = [picked_s, v_scale1]
+
+        def move_scale_rows(a):
+            for q in range(4):
+                row = 16 * a + 4 * q
+                nc.sync.dma_start(
+                    v_scale[32 * q : 32 * q + 4, a, :].bitcast(I32),
+                    picked_s[row : row + 4, :].bitcast(I32),
+                )
+
+        tab_w = [held([P, T], I32, "tab_w%d" % a) for a in range(2)]
+        w1_first = held([P, PACK, M], F32, "w1_first")
+        w1_last = [held([P, PACK, M // 2], F32, "w1_raw1%d" % u) for u in range(2)]
+        nc.sync.dma_start(tab_w[0][:], tab_rows[0])
+        nc.sync.dma_start(w1_first[:], w1_rows[0])
+        nc.sync.dma_start(tab_w[1][:], tab_rows[1])
+        move_scale_rows(0)
+        for u in range(2):
+            nc.sync.dma_start(w1_last[u][:], w1_rows[1][:, :, u * 256 : (u + 1) * 256])
+        move_scale_rows(1)
+        w1_raw = [w1_first[:, :, 0:256], w1_first[:, :, 256:512], w1_last[0][:], w1_last[1][:]]
 
         w3_c = held([P, 2, 2 * H], U8, "w3_c")
         nc.vector.tensor_copy(
@@ -129,7 +114,8 @@ def tile_list_panel_node_features_kernel(
         v_words = [[None, None], [None, None]]
 
         def pick_table(a, u):
-            tile = held([P, HALF], I32, "v_words%d%d" % (a, u))
+            name = "v_words%d%d" % (a, u)
+            tile = held([P, HALF], I32, name, tag="w1_b1" if (a, u) == (1, 1) else name)
             nc.vector.tensor_copy(
                 tile[:].bitcast(U32),
                 tab_w[a][:].bitcast(U32).indirect(list_slice(lists["offs"], u * HALF, HALF)),
@@ -144,10 +130,10 @@ def tile_list_panel_node_features_kernel(
         w1_b = [held([P, PACK, P, PACK], BF16, "w1_b%d" % a) for a in range(2)]
         for a in range(2):
             for u in range(2):
-                copy = nc.vector.tensor_copy if (a, u) in ((1, 1),) else nc.scalar.copy
+                copy = nc.vector.tensor_copy if (a, u) in ((0, 1), (1, 1)) else nc.scalar.copy
                 copy(
                     w1_b[a][:, :, 64 * u : 64 * (u + 1), :].rearrange("p t q j -> p q j t"),
-                    w1_raw[2 * a + u][:].rearrange("p j (q t) -> p q j t", t=PACK),
+                    w1_raw[2 * a + u].rearrange("p j (q t) -> p q j t", t=PACK),
                 )
             nc.vector.quantize_mx(
                 out=w1_c[:, a, :].bitcast(FP8X4), scales=w1_s[:, a, :],
@@ -164,7 +150,7 @@ def tile_list_panel_node_features_kernel(
         def second_reading(first):
             u, c0 = divmod(first, HALF)
             for pair in range(2):
-                acc = bank("pa", 2, "acc3")
+                acc = bank("pa", 4, "acc3")
                 for s in range(2):
                     t = 2 * pair + s
                     for n0 in range(0, CHUNK, P):
@@ -174,7 +160,7 @@ def tile_list_panel_node_features_kernel(
                                 lhsT=w3_c[:, a, t * 256 : (t + 1) * 256].bitcast(FP4X4),
                                 lhsT_scale=w3_s[:, a, t * P : (t + 1) * P],
                                 rhs=v_words[a][u][:, c0 + n0 : c0 + n0 + P].bitcast(FP8X4),
-                                rhs_scale=v_plane[a][:, first + n0 : first + n0 + P],
+                                rhs_scale=v_scale[:, a, first + n0 : first + n0 + P],
                                 start=(a == 0), stop=(a == 1),
                             )
                 nc.scalar.copy(
@@ -184,6 +170,15 @@ def tile_list_panel_node_features_kernel(
 
         w2_raw = held([P, H], I32, "w2_raw")
         nc.sync.dma_start(w2_raw[:], w2_words[0].rearrange("p c i -> p (c i)").bitcast(I32))
+        for q in range(4):
+            nc.sync.dma_start(
+                wsc_raw[32 * q : 32 * q + 4, 2, :].bitcast(I32),
+                w2_scales[0, 4 * q : 4 * q + 4, :].bitcast(I32),
+            )
+        gm_col = held([P, PACK], F32, "gm_col")
+        nc.sync.dma_start(gm_col[:], gm.rearrange("(p t) -> p t", t=PACK))
+        gm2 = held([P, PACK], F32, "gm2")
+        nc.vector.tensor_scalar(gm2[:], gm_col[:], 2.0, None, ALU.mult)
         page_rows = page0.rearrange("(p t) c -> t p c", t=PACK)
         wgs_rows = wgs.rearrange("(q t) j -> q t j", t=PACK)
         page = [
@@ -211,6 +206,11 @@ def tile_list_panel_node_features_kernel(
         load_gain(HALF, HALF)
         nc.sync.dma_start(lists["offs3"][:], offs3)
         nc.sync.dma_start(lists["offs4"][:], offs4)
+        gs_col = held([P, PACK], F32, "gs_col")
+        gx_col = held([P, PACK], F32, "gx_col")
+        gg_col = held([P, PACK], F32, "gg_col")
+        for tile, vec in ((gs_col, gs), (gx_col, gx), (gg_col, gg)):
+            nc.sync.dma_start(tile[:], vec.rearrange("(p t) -> p t", t=PACK))
         w4_raw = held([P, PACK, H], F32, "w4_raw")
         nc.sync.dma_start(w4_raw[:], w4.rearrange("(p j) n -> p j n", j=PACK))
 
@@ -242,9 +242,11 @@ def tile_list_panel_node_features_kernel(
             first = c * CHUNK
             u, c0 = divmod(first, HALF)
             cols = slice(first, first + CHUNK)
+            if c == 0:
+                second_reading(first)
             gel = ring.tile([P, PACK, CHUNK], F32, name="gel", tag="gel", align_bytes=64)
             for pair in range(2):
-                acc = bank("pb", 3, "acc1")
+                acc = bank("pa", 4, "acc1")
                 for s in range(2):
                     t = 2 * pair + s
                     for a in range(2):
@@ -253,14 +255,15 @@ def tile_list_panel_node_features_kernel(
                             lhsT=w1_c[:, a, t * P : (t + 1) * P].bitcast(FP8X4),
                             lhsT_scale=w1_s[:, a, t * P : (t + 1) * P],
                             rhs=v_words[a][u][:, c0 : c0 + CHUNK].bitcast(FP8X4),
-                            rhs_scale=picked_s[4 * a : P, cols],
+                            rhs_scale=v_scale[:, a, cols],
                             start=(a == 0), stop=(a == 1),
                         )
                 nc.scalar.activation(
                     gel[:, 2 * pair : 2 * pair + 2, :].rearrange("p s n -> p (s n)"),
                     acc[:], ACT.Gelu_apprx_tanh,
                 )
-            second_reading(first)
+            if c > 0:
+                second_reading(first)
             if c == 0:
                 pick_table(0, 1)
                 pick_table(1, 1)
@@ -286,6 +289,8 @@ def tile_list_panel_node_features_kernel(
                 out=a_c[:].bitcast(FP8X4), scales=a_s[:, cols],
                 in_=a_b[:].rearrange("p n t -> p (n t)"),
             )
+            if c > 0:
+                scatter(first - CHUNK, (2, 3))
             for pair in range(2):
                 acc = bank("pc", 3, "acc2")
                 for s in range(2):
@@ -310,13 +315,15 @@ def tile_list_panel_node_features_kernel(
                     ALU.min,
                 )
             if c < S // CHUNK - 1:
-                scatter(first, range(PACK))
+                scatter(first, (0, 1))
 
         w4_b = held([P, PACK, P, PACK], BF16, "w4_b", tag="a_rows")
         nc.scalar.copy(
             w4_b[:].rearrange("p t q j -> p q j t"),
             w4_raw[:].rearrange("p j (q t) -> p q j t", t=PACK),
         )
+        gg_neg = held([P, PACK], F32, "gg_neg")
+        nc.scalar.activation(gg_neg[:], gg_col[:], ACT.Copy, scale=-1.0)
         w4_c = held([P, H], U32, "w4_c")
         w4_s = held([P, H], U8, "w4_s")
         nc.vector.quantize_mx(
@@ -324,7 +331,7 @@ def tile_list_panel_node_features_kernel(
             in_=w4_b[:].rearrange("p t q j -> p (t q j)"),
         )
 
-        x_rows = [held([P, PACK, HALF], BF16, "x_rows%d" % u, tag="w1_raw0%d" % u) for u in range(2)]
+        x_rows = [held([P, PACK, HALF], BF16, "x_rows%d" % u) for u in range(2)]
 
         def reread(t):
             pieces = 2 if t == PACK - 1 else 1
@@ -380,7 +387,7 @@ def tile_list_panel_node_features_kernel(
                     page[t][:].indirect(list_slice(lists["offs4"], u * HALF, HALF)),
                 )
             for t in range(PACK):
-                acc = bank("pa", 2, "acc4") if t % 2 == 0 else bank("pb", 3, "acc4")
+                acc = bank("pa", 4, "acc4")
                 nc.tensor.matmul_mx(
                     out=acc[:],
                     lhsT=w4_c[:, t * P : (t + 1) * P].bitcast(FP8X4),

@@ -50,8 +50,8 @@ def tile_list_panel_node_features_kernel(
         def held(shape, dtype, name, tag=None):
             return keep.tile(shape, dtype, name=name, tag=tag or name, align_bytes=64)
 
-        def bank(tag, bufs, name):
-            return psum.tile([P, HALF], F32, name=name, tag=tag, bufs=bufs)
+        def bank(tag, name):
+            return psum.tile([P, HALF], F32, name=name, tag=tag, bufs=2)
 
         lists = {}
         for name in ("offs", "offs2", "offs3", "offs4"):
@@ -94,16 +94,13 @@ def tile_list_panel_node_features_kernel(
                 )
 
         tab_w = [held([P, T], I32, "tab_w%d" % a) for a in range(2)]
-        w1_first = held([P, PACK, M], F32, "w1_first")
-        w1_last = [held([P, PACK, M // 2], F32, "w1_raw1%d" % u) for u in range(2)]
+        w1_raw = [held([P, PACK, M], F32, "w1_raw%d" % a) for a in range(2)]
         nc.sync.dma_start(tab_w[0][:], tab_rows[0])
-        nc.sync.dma_start(w1_first[:], w1_rows[0])
+        nc.sync.dma_start(w1_raw[0][:], w1_rows[0])
         nc.sync.dma_start(tab_w[1][:], tab_rows[1])
         move_scale_rows(0)
-        for u in range(2):
-            nc.sync.dma_start(w1_last[u][:], w1_rows[1][:, :, u * 256 : (u + 1) * 256])
+        nc.sync.dma_start(w1_raw[1][:], w1_rows[1])
         move_scale_rows(1)
-        w1_raw = [w1_first[:, :, 0:256], w1_first[:, :, 256:512], w1_last[0][:], w1_last[1][:]]
 
         w3_c = held([P, 2, 2 * H], U8, "w3_c")
         nc.vector.tensor_copy(
@@ -114,8 +111,7 @@ def tile_list_panel_node_features_kernel(
         v_words = [[None, None], [None, None]]
 
         def pick_table(a, u):
-            name = "v_words%d%d" % (a, u)
-            tile = held([P, HALF], I32, name, tag="w1_b1" if (a, u) == (1, 1) else name)
+            tile = held([P, HALF], I32, "v_words%d%d" % (a, u))
             nc.vector.tensor_copy(
                 tile[:].bitcast(U32),
                 tab_w[a][:].bitcast(U32).indirect(list_slice(lists["offs"], u * HALF, HALF)),
@@ -129,11 +125,10 @@ def tile_list_panel_node_features_kernel(
         w1_s = held([P, 2, M], U8, "w1_s")
         w1_b = [held([P, PACK, P, PACK], BF16, "w1_b%d" % a) for a in range(2)]
         for a in range(2):
-            for u in range(2):
-                copy = nc.vector.tensor_copy if (a, u) in ((0, 1), (1, 1)) else nc.scalar.copy
+            for copy, q0, q1 in ((nc.scalar.copy, 0, 40), (nc.vector.tensor_copy, 40, P)):
                 copy(
-                    w1_b[a][:, :, 64 * u : 64 * (u + 1), :].rearrange("p t q j -> p q j t"),
-                    w1_raw[2 * a + u].rearrange("p j (q t) -> p q j t", t=PACK),
+                    w1_b[a][:, :, q0:q1, :].rearrange("p t q j -> p q j t"),
+                    w1_raw[a][:, :, PACK * q0 : PACK * q1].rearrange("p j (q t) -> p q j t", t=PACK),
                 )
             nc.vector.quantize_mx(
                 out=w1_c[:, a, :].bitcast(FP8X4), scales=w1_s[:, a, :],
@@ -150,7 +145,7 @@ def tile_list_panel_node_features_kernel(
         def second_reading(first):
             u, c0 = divmod(first, HALF)
             for pair in range(2):
-                acc = bank("pa", 4, "acc3")
+                acc = bank(("pa", "pd", "pd", "pc")[first // CHUNK], "acc3")
                 for s in range(2):
                     t = 2 * pair + s
                     for n0 in range(0, CHUNK, P):
@@ -200,9 +195,11 @@ def tile_list_panel_node_features_kernel(
         nc.sync.dma_start(lists["offs2"][:], offs2)
         load_gain(0, CHUNK)
         nc.sync.dma_start(page[1][:], page_rows[1])
-        load_gain(CHUNK, CHUNK)
         nc.sync.dma_start(page[2][:], page_rows[2])
         nc.sync.dma_start(page[3][:], page_rows[3])
+        load_gain(CHUNK, CHUNK)
+        w4_raw = held([P, PACK, H], F32, "w4_raw")
+        nc.sync.dma_start(w4_raw[:], w4.rearrange("(p j) n -> p j n", j=PACK))
         load_gain(HALF, HALF)
         nc.sync.dma_start(lists["offs3"][:], offs3)
         nc.sync.dma_start(lists["offs4"][:], offs4)
@@ -211,8 +208,6 @@ def tile_list_panel_node_features_kernel(
         gg_col = held([P, PACK], F32, "gg_col")
         for tile, vec in ((gs_col, gs), (gx_col, gx), (gg_col, gg)):
             nc.sync.dma_start(tile[:], vec.rearrange("(p t) -> p t", t=PACK))
-        w4_raw = held([P, PACK, H], F32, "w4_raw")
-        nc.sync.dma_start(w4_raw[:], w4.rearrange("(p j) n -> p j n", j=PACK))
 
         w2_c = held([P, H], I32, "w2_c")
         w2_s = held([P, H], U8, "w2_s")
@@ -246,7 +241,7 @@ def tile_list_panel_node_features_kernel(
                 second_reading(first)
             gel = ring.tile([P, PACK, CHUNK], F32, name="gel", tag="gel", align_bytes=64)
             for pair in range(2):
-                acc = bank("pa", 4, "acc1")
+                acc = bank(("pb", "pa", "pb", "pc")[c], "acc1")
                 for s in range(2):
                     t = 2 * pair + s
                     for a in range(2):
@@ -262,8 +257,6 @@ def tile_list_panel_node_features_kernel(
                     gel[:, 2 * pair : 2 * pair + 2, :].rearrange("p s n -> p (s n)"),
                     acc[:], ACT.Gelu_apprx_tanh,
                 )
-            if c > 0:
-                second_reading(first)
             if c == 0:
                 pick_table(0, 1)
                 pick_table(1, 1)
@@ -290,9 +283,10 @@ def tile_list_panel_node_features_kernel(
                 in_=a_b[:].rearrange("p n t -> p (n t)"),
             )
             if c > 0:
+                second_reading(first)
                 scatter(first - CHUNK, (2, 3))
             for pair in range(2):
-                acc = bank("pc", 3, "acc2")
+                acc = bank(("pd", "pc", "pd", "pc")[c], "acc2")
                 for s in range(2):
                     t = 2 * pair + s
                     nc.tensor.matmul_mx(
@@ -324,14 +318,14 @@ def tile_list_panel_node_features_kernel(
         )
         gg_neg = held([P, PACK], F32, "gg_neg")
         nc.scalar.activation(gg_neg[:], gg_col[:], ACT.Copy, scale=-1.0)
-        w4_c = held([P, H], U32, "w4_c")
+        w4_c = slide.tile([P, H], U32, name="w4_c", offset=3 * KB, align_bytes=64)
         w4_s = held([P, H], U8, "w4_s")
         nc.vector.quantize_mx(
             out=w4_c[:].bitcast(FP8X4), scales=w4_s[:],
             in_=w4_b[:].rearrange("p t q j -> p (t q j)"),
         )
 
-        x_rows = [held([P, PACK, HALF], BF16, "x_rows%d" % u) for u in range(2)]
+        x_rows = [held([P, PACK, HALF], BF16, "x_rows%d" % u, tag="w1_raw%d" % u) for u in range(2)]
 
         def reread(t):
             pieces = 2 if t == PACK - 1 else 1
@@ -343,7 +337,7 @@ def tile_list_panel_node_features_kernel(
                     picked[:, cols],
                     page[t][:].indirect(list_slice(lists["offs3"], piece * width, width)),
                 )
-                sine = ring.tile([P, width], F32, name="sine", tag="gel", align_bytes=64)
+                sine = held([P, width], F32, "sine")
                 nc.scalar.activation(sine[:], picked[:, cols], ACT.Sin, scale=gs_col[:, t : t + 1])
                 for u in range(2) if pieces == 1 else [piece]:
                     c0 = u * HALF - piece * width
@@ -361,21 +355,21 @@ def tile_list_panel_node_features_kernel(
         x_c = held([P, NP], U32, "x_c")
         x_s = held([P, NP], U8, "x_s")
         y = held([P, PACK, NP], F32, "y", tag="h3")
-        y_c = held([P, NP], I32, "y_c")
+        y_b = []
         y_s = held([P, NP], U8, "y_s")
         out_rows = out_0.rearrange("(p t) j -> t p j", t=PACK)
         out_words = out_1[0].rearrange("p m t -> p (m t)").bitcast(I32)
         for u in range(2):
             cols = slice(u * HALF, (u + 1) * HALF)
-            x_b = held([P, HALF, PACK], BF16, "x_b%d" % u, tag="w1_raw1%d" % u)
+            x_b = held([P, HALF, PACK], BF16, "x_b%d" % u, tag="x_b%d" % u)
             nc.scalar.copy(weave_out(x_b[:]), weave_in(x_rows[u][:]))
             if u == 0:
                 whole = held([P, PACK, HALF], F32, "golden0", tag="gain2")
                 golden = [whole[:, t, :] for t in range(PACK)]
             else:
                 early = held([P, 2, HALF], F32, "golden1a")
-                late = held([P, 1, HALF], F32, "golden1b", tag="w1_raw10")
-                last = held([P, HALF], F32, "golden1c", tag="w1_raw11")
+                late = held([P, 1, HALF], F32, "golden1b", tag="x_b0")
+                last = held([P, HALF], F32, "golden1c", tag="x_b1")
                 golden = [early[:, t, :] for t in range(2)] + [late[:, t, :] for t in range(1)] + [last[:]]
             nc.vector.quantize_mx(
                 out=x_c[:, cols].bitcast(FP8X4), scales=x_s[:, cols],
@@ -387,7 +381,7 @@ def tile_list_panel_node_features_kernel(
                     page[t][:].indirect(list_slice(lists["offs4"], u * HALF, HALF)),
                 )
             for t in range(PACK):
-                acc = bank("pa", 4, "acc4")
+                acc = bank(("pa", "pb")[t % 2], "acc4")
                 nc.tensor.matmul_mx(
                     out=acc[:],
                     lhsT=w4_c[:, t * P : (t + 1) * P].bitcast(FP8X4),
@@ -401,21 +395,23 @@ def tile_list_panel_node_features_kernel(
                     ALU.mult, ALU.add,
                 )
                 nc.sync.dma_start(out_rows[t][:, cols], y[:, t, cols])
-            y_b = held([P, HALF, PACK], BF16, "y_b%d" % u, tag="w1_b%d" % u)
+            y_b.append(held([P, HALF, PACK], BF16, "y_b%d" % u, tag="w1_b%d" % u))
             if u == 0:
-                nc.scalar.copy(weave_out(y_b[:]), weave_in(y[:, :, cols]))
-            else:
-                nc.scalar.copy(
-                    weave_out(y_b[:, 0:CHUNK, :]), weave_in(y[:, :, HALF : HALF + CHUNK])
-                )
+                nc.scalar.copy(weave_out(y_b[u][:]), weave_in(y[:, :, cols]))
+        split = 192
+        nc.scalar.copy(weave_out(y_b[1][:, 0:split, :]), weave_in(y[:, :, HALF : HALF + split]))
+        for u in range(2):
+            cols = slice(u * HALF, (u + 1) * HALF)
+            if u == 1:
                 nc.vector.tensor_copy(
-                    weave_out(y_b[:, CHUNK:HALF, :]), weave_in(y[:, :, HALF + CHUNK : NP])
+                    weave_out(y_b[1][:, split:HALF, :]), weave_in(y[:, :, HALF + split : NP])
                 )
+            y_c = held([P, HALF], I32, "y_c%d" % u, tag="x_b1" if u == 0 else None)
             nc.vector.quantize_mx(
-                out=y_c[:, cols].bitcast(FP8X4), scales=y_s[:, cols],
-                in_=y_b[:].rearrange("p n t -> p (n t)"),
+                out=y_c[:].bitcast(FP8X4), scales=y_s[:, cols],
+                in_=y_b[u][:].rearrange("p n t -> p (n t)"),
             )
-            nc.sync.dma_start(out_words[:, cols], y_c[:, cols])
+            nc.sync.dma_start(out_words[:, cols], y_c[:])
         for q in range(4):
             (nc.scalar if q % 2 == 0 else nc.sync).dma_start(
                 out_2[0, 4 * q : 4 * q + 4, :].bitcast(I32),

@@ -17,11 +17,23 @@ ALU = mybir.AluOpType
 ACT = mybir.ActivationFunctionType
 
 P = 128
-PACK = 4
+SLOTS = 4
+PASSES = K // (P * SLOTS)
+QUADRANT = 32
 HALF = 512
 CHUNK = 256
+CHUNKS = S // CHUNK
 LIST_ROWS = 16
 KB = 1024
+
+W1_ON_SCALAR = 40
+Y_ON_SCALAR = 192
+
+H_AT = (0, KB, 5 * KB, 9 * KB)
+
+BANKS_B = "BABC"
+BANKS_SECOND = "ADDC"
+BANKS_FIRST = "DCDC"
 
 
 def list_slice(offsets, first, count):
@@ -36,6 +48,10 @@ def weave_in(tile):
     return tile.rearrange("p t (c i) -> p c t i", i=4)
 
 
+def slot(t):
+    return slice(t * P, (t + 1) * P)
+
+
 def tile_list_panel_node_features_kernel(
     tc, tab_words, tab_scales, offs, w1, gm, w2_words, w2_scales, w3_words, w3_scales,
     wgs, page0, offs2, offs3, gs, gx, w4, offs4, gg, out_0, out_1, out_2,
@@ -43,123 +59,132 @@ def tile_list_panel_node_features_kernel(
     nc = tc.nc
     with ExitStack() as ctx:
         keep = ctx.enter_context(tc.tile_pool(name="keep", bufs=1))
-        slide = ctx.enter_context(tc.tile_pool(name="slide", bufs=1))
+        staged = ctx.enter_context(tc.tile_pool(name="staged", bufs=1))
         ring = ctx.enter_context(tc.tile_pool(name="ring", bufs=2))
         psum = ctx.enter_context(tc.psum_pool(name="psum", bufs=1))
 
-        def held(shape, dtype, name, tag=None):
-            return keep.tile(shape, dtype, name=name, tag=tag or name, align_bytes=64)
+        def held(shape, dtype, name, after=None):
+            return keep.tile(shape, dtype, name=name, tag=after or name, align_bytes=64)
 
-        def bank(tag, name):
-            return psum.tile([P, HALF], F32, name=name, tag=tag, bufs=2)
+        def placed(shape, dtype, name, offset):
+            return staged.tile(shape, dtype, name=name, offset=offset, align_bytes=64)
+
+        def bank(pair, name):
+            return psum.tile([P, HALF], F32, name=name, tag=pair, bufs=2)
+
+        def gelu_tile(columns):
+            return ring.tile([P, SLOTS, columns], F32, name="gel", align_bytes=64)
 
         lists = {}
         for name in ("offs", "offs2", "offs3", "offs4"):
             lists[name] = held([P, S // LIST_ROWS], U16, "list_" + name)
 
         tab_s = held([P, T], U8, "tab_s")
-        wsc_raw = held([P, 3, H], U8, "wsc_raw")
-        v_scale = held([P, 2, S], U8, "v_scale")
+        w_s_raw = held([P, PASSES + 1, H], U8, "w_s_raw")
+        v_s = held([P, PASSES, S], U8, "v_s")
         warm = held([P, 1], F32, "warm")
-        nc.vector.memset(wsc_raw[:].rearrange("p a c -> p (a c)").bitcast(I32), 0)
+        nc.vector.memset(w_s_raw[:].rearrange("p a c -> p (a c)").bitcast(I32), 0)
         nc.vector.memset(tab_s[32:64, :].bitcast(I32), 0)
         nc.vector.memset(tab_s[64:128, :].bitcast(I32), 0)
-        nc.vector.memset(v_scale[:].rearrange("p a c -> p (a c)").bitcast(I32), 0)
+        nc.vector.memset(v_s[:].rearrange("p a c -> p (a c)").bitcast(I32), 0)
 
         nc.sync.dma_start(
             tab_s[0:32, :].bitcast(I32), tab_scales.rearrange("a q t -> (a q) t").bitcast(I32)
         )
         nc.sync.dma_start(lists["offs"][:], offs)
-        w3_raw = held([P, 2, 2 * H], U8, "w3_raw")
+        w3_raw = held([P, PASSES, 2 * H], U8, "w3_raw")
         nc.sync.dma_start(w3_raw[:].bitcast(I32), w3_words.rearrange("a p b -> p a b").bitcast(I32))
         for q in range(4):
             nc.scalar.dma_start(
-                wsc_raw[32 * q : 32 * q + 4, 0:2, :].bitcast(I32),
+                w_s_raw[QUADRANT * q : QUADRANT * q + 4, 0:PASSES, :].bitcast(I32),
                 w3_scales[:, 4 * q : 4 * q + 4, :].rearrange("a r c -> r a c").bitcast(I32),
             )
         nc.vector.memset(warm[:], 0.0)
         warm_out = held([P, 1], F32, "warm_out")
         nc.scalar.activation(warm_out[:], warm[:], ACT.Gelu_apprx_tanh)
-        tab_rows = tab_words.rearrange("a p t i -> a p (t i)").bitcast(I32)
-        w1_rows = w1.rearrange("(a p j) m -> a p j m", a=2, j=PACK)
+
         picked_s = held([P, S], U8, "picked_s")
         nc.vector.tensor_copy(picked_s[:], tab_s[:].indirect(lists["offs"][:]))
 
-        def move_scale_rows(a):
+        def move_scale_rows(a, queue):
             for q in range(4):
                 row = 16 * a + 4 * q
-                nc.sync.dma_start(
-                    v_scale[32 * q : 32 * q + 4, a, :].bitcast(I32),
+                queue.dma_start(
+                    v_s[QUADRANT * q : QUADRANT * q + 4, a, :].bitcast(I32),
                     picked_s[row : row + 4, :].bitcast(I32),
                 )
 
-        tab_w = [held([P, T], I32, "tab_w%d" % a) for a in range(2)]
-        w1_raw = [held([P, PACK, M], F32, "w1_raw%d" % a) for a in range(2)]
+        tab_rows = tab_words.rearrange("a p t i -> a p (t i)").bitcast(I32)
+        w1_rows = w1.rearrange("(a p j) m -> a p j m", a=PASSES, j=SLOTS)
+        tab_w = [held([P, T], I32, "tab_w%d" % a) for a in range(PASSES)]
+        w1_raw = [held([P, SLOTS, M], F32, "w1_raw%d" % a) for a in range(PASSES)]
         nc.sync.dma_start(tab_w[0][:], tab_rows[0])
         nc.sync.dma_start(w1_raw[0][:], w1_rows[0])
         nc.sync.dma_start(tab_w[1][:], tab_rows[1])
-        move_scale_rows(0)
+        move_scale_rows(0, nc.sync)
         nc.sync.dma_start(w1_raw[1][:], w1_rows[1])
-        move_scale_rows(1)
+        move_scale_rows(1, nc.gpsimd)
 
-        w3_c = held([P, 2, 2 * H], U8, "w3_c")
+        w3_c = held([P, PASSES, 2 * H], U8, "w3_c")
         nc.vector.tensor_copy(
-            w3_c[:].bitcast(U16).rearrange("p a (t q) -> p a q t", t=PACK),
-            w3_raw[:].bitcast(U16).rearrange("p a (q t) -> p a q t", t=PACK),
+            w3_c[:].bitcast(U16).rearrange("p a (t q) -> p a q t", t=SLOTS),
+            w3_raw[:].bitcast(U16).rearrange("p a (q t) -> p a q t", t=SLOTS),
         )
 
-        v_words = [[None, None], [None, None]]
+        v_c = {}
 
-        def pick_table(a, u):
-            tile = held([P, HALF], I32, "v_words%d%d" % (a, u))
-            nc.vector.tensor_copy(
-                tile[:].bitcast(U32),
-                tab_w[a][:].bitcast(U32).indirect(list_slice(lists["offs"], u * HALF, HALF)),
-            )
-            v_words[a][u] = tile
+        def pick_words(half):
+            for a in range(PASSES):
+                words = held([P, HALF], I32, "v_c%d%d" % (a, half))
+                nc.vector.tensor_copy(
+                    words[:].bitcast(U32),
+                    tab_w[a][:].bitcast(U32).indirect(list_slice(lists["offs"], half * HALF, HALF)),
+                )
+                v_c[a, half] = words
 
-        pick_table(0, 0)
-        pick_table(1, 0)
+        pick_words(0)
 
-        w1_c = held([P, 2, M], U32, "w1_c")
-        w1_s = held([P, 2, M], U8, "w1_s")
-        w1_b = [held([P, PACK, P, PACK], BF16, "w1_b%d" % a) for a in range(2)]
-        for a in range(2):
-            for copy, q0, q1 in ((nc.scalar.copy, 0, 40), (nc.vector.tensor_copy, 40, P)):
+        w1_c = held([P, PASSES, M], U32, "w1_c")
+        w1_s = held([P, PASSES, M], U8, "w1_s")
+        w1_b = [held([P, SLOTS, P, SLOTS], BF16, "w1_b%d" % a) for a in range(PASSES)]
+        shares = ((nc.scalar.copy, 0, W1_ON_SCALAR), (nc.vector.tensor_copy, W1_ON_SCALAR, P))
+        for a in range(PASSES):
+            for copy, q0, q1 in shares:
                 copy(
                     w1_b[a][:, :, q0:q1, :].rearrange("p t q j -> p q j t"),
-                    w1_raw[a][:, :, PACK * q0 : PACK * q1].rearrange("p j (q t) -> p q j t", t=PACK),
+                    w1_raw[a][:, :, SLOTS * q0 : SLOTS * q1].rearrange("p j (q t) -> p q j t", t=SLOTS),
                 )
             nc.vector.quantize_mx(
                 out=w1_c[:, a, :].bitcast(FP8X4), scales=w1_s[:, a, :],
                 in_=w1_b[a][:].rearrange("p t q j -> p (t q j)"),
             )
-        w3_s = held([P, 2, H], U8, "w3_s")
+        w3_s = held([P, PASSES, H], U8, "w3_s")
         nc.vector.tensor_copy(
-            w3_s[:].rearrange("p a (t q) -> p a q t", t=PACK),
-            wsc_raw[:, 0:2, :].rearrange("p a (q t) -> p a q t", t=PACK),
+            w3_s[:].rearrange("p a (t q) -> p a q t", t=SLOTS),
+            w_s_raw[:, 0:PASSES, :].rearrange("p a (q t) -> p a q t", t=SLOTS),
         )
 
-        h3 = held([P, PACK, S], F32, "h3", tag="h3")
+        second = held([P, SLOTS, S], F32, "second", after="w1_raw1")
 
-        def second_reading(first):
-            u, c0 = divmod(first, HALF)
+        def second_reading(c):
+            first = c * CHUNK
+            half, c0 = divmod(first, HALF)
             for pair in range(2):
-                acc = bank(("pa", "pd", "pd", "pc")[first // CHUNK], "acc3")
+                acc = bank(BANKS_SECOND[c], "acc_second")
                 for s in range(2):
                     t = 2 * pair + s
                     for n0 in range(0, CHUNK, P):
-                        for a in range(2):
+                        for a in range(PASSES):
                             nc.tensor.matmul_mx(
                                 out=acc[:, s * CHUNK + n0 : s * CHUNK + n0 + P],
-                                lhsT=w3_c[:, a, t * 256 : (t + 1) * 256].bitcast(FP4X4),
-                                lhsT_scale=w3_s[:, a, t * P : (t + 1) * P],
-                                rhs=v_words[a][u][:, c0 + n0 : c0 + n0 + P].bitcast(FP8X4),
-                                rhs_scale=v_scale[:, a, first + n0 : first + n0 + P],
-                                start=(a == 0), stop=(a == 1),
+                                lhsT=w3_c[:, a, 2 * t * P : 2 * (t + 1) * P].bitcast(FP4X4),
+                                lhsT_scale=w3_s[:, a, slot(t)],
+                                rhs=v_c[a, half][:, c0 + n0 : c0 + n0 + P].bitcast(FP8X4),
+                                rhs_scale=v_s[:, a, first + n0 : first + n0 + P],
+                                start=(a == 0), stop=(a == PASSES - 1),
                             )
                 nc.scalar.copy(
-                    h3[:, 2 * pair : 2 * pair + 2, first : first + CHUNK],
+                    second[:, 2 * pair : 2 * pair + 2, first : first + CHUNK],
                     acc[:].rearrange("p (s n) -> p s n", s=2),
                 )
 
@@ -167,253 +192,274 @@ def tile_list_panel_node_features_kernel(
         nc.sync.dma_start(w2_raw[:], w2_words[0].rearrange("p c i -> p (c i)").bitcast(I32))
         for q in range(4):
             nc.sync.dma_start(
-                wsc_raw[32 * q : 32 * q + 4, 2, :].bitcast(I32),
+                w_s_raw[QUADRANT * q : QUADRANT * q + 4, PASSES, :].bitcast(I32),
                 w2_scales[0, 4 * q : 4 * q + 4, :].bitcast(I32),
             )
-        gm_col = held([P, PACK], F32, "gm_col")
-        nc.sync.dma_start(gm_col[:], gm.rearrange("(p t) -> p t", t=PACK))
-        gm2 = held([P, PACK], F32, "gm2")
+        gm_col = held([P, SLOTS], F32, "gm_col")
+        nc.sync.dma_start(gm_col[:], gm.rearrange("(p t) -> p t", t=SLOTS))
+        gm2 = held([P, SLOTS], F32, "gm2")
         nc.vector.tensor_scalar(gm2[:], gm_col[:], 2.0, None, ALU.mult)
-        page_rows = page0.rearrange("(p t) c -> t p c", t=PACK)
-        wgs_rows = wgs.rearrange("(q t) j -> q t j", t=PACK)
-        page = [
-            held([P, T2], F32, "page%d" % t) for t in range(PACK)
-        ]
+
+        page_rows = page0.rearrange("(p t) c -> t p c", t=SLOTS)
+        wgs_rows = wgs.rearrange("(i t) j -> i t j", t=SLOTS)
+        page = [held([P, T2], F32, "page%d" % t) for t in range(SLOTS)]
         gain = {
-            0: held([P, PACK, CHUNK], F32, "gain0"),
-            CHUNK: held([P, PACK, CHUNK], F32, "gain1"),
-            HALF: held([P, PACK, HALF], F32, "gain2"),
+            0: held([P, SLOTS, CHUNK], F32, "gain0"),
+            CHUNK: held([P, SLOTS, CHUNK], F32, "gain1"),
+            HALF: held([P, SLOTS, HALF], F32, "gain2"),
         }
 
         def load_gain(first, count):
             for q in (0, 2, 1, 3):
                 nc.sync.dma_start(
-                    gain[first][32 * q : 32 * q + 32, :, :], wgs_rows[:, :, first : first + count]
+                    gain[first][QUADRANT * q : QUADRANT * (q + 1), :, :],
+                    wgs_rows[:, :, first : first + count],
                 )
 
         nc.sync.dma_start(page[0][:], page_rows[0])
         nc.sync.dma_start(lists["offs2"][:], offs2)
         load_gain(0, CHUNK)
-        nc.sync.dma_start(page[1][:], page_rows[1])
-        nc.sync.dma_start(page[2][:], page_rows[2])
-        nc.sync.dma_start(page[3][:], page_rows[3])
+        for t in range(1, SLOTS):
+            nc.sync.dma_start(page[t][:], page_rows[t])
         load_gain(CHUNK, CHUNK)
-        w4_raw = held([P, PACK, H], F32, "w4_raw")
-        nc.sync.dma_start(w4_raw[:], w4.rearrange("(p j) n -> p j n", j=PACK))
+        w4_raw = held([P, SLOTS, H], F32, "w4_raw")
+        nc.sync.dma_start(w4_raw[:], w4.rearrange("(p j) n -> p j n", j=SLOTS))
         load_gain(HALF, HALF)
         nc.sync.dma_start(lists["offs3"][:], offs3)
         nc.sync.dma_start(lists["offs4"][:], offs4)
-        gs_col = held([P, PACK], F32, "gs_col")
-        gx_col = held([P, PACK], F32, "gx_col")
-        gg_col = held([P, PACK], F32, "gg_col")
-        for tile, vec in ((gs_col, gs), (gx_col, gx), (gg_col, gg)):
-            nc.sync.dma_start(tile[:], vec.rearrange("(p t) -> p t", t=PACK))
+        gs_col = held([P, SLOTS], F32, "gs_col")
+        gx_col = held([P, SLOTS], F32, "gx_col")
+        gg_col = held([P, SLOTS], F32, "gg_col")
+        for column, vec in ((gs_col, gs), (gx_col, gx), (gg_col, gg)):
+            nc.sync.dma_start(column[:], vec.rearrange("(p t) -> p t", t=SLOTS))
 
-        w2_c = held([P, H], I32, "w2_c")
+        w2_c = held([P, H], I32, "w2_c", after="w1_b1")
         w2_s = held([P, H], U8, "w2_s")
         nc.vector.tensor_copy(
-            w2_c[:].rearrange("p (t q) -> p q t", t=PACK),
-            w2_raw[:].rearrange("p (q t) -> p q t", t=PACK),
+            w2_c[:].rearrange("p (t q) -> p q t", t=SLOTS),
+            w2_raw[:].rearrange("p (q t) -> p q t", t=SLOTS),
         )
         nc.vector.tensor_copy(
-            w2_s[:].rearrange("p (t q) -> p q t", t=PACK),
-            wsc_raw[:, 2, :].rearrange("p (q t) -> p q t", t=PACK),
+            w2_s[:].rearrange("p (t q) -> p q t", t=SLOTS),
+            w_s_raw[:, PASSES, :].rearrange("p (q t) -> p q t", t=SLOTS),
         )
 
         a_s = held([P, S], U8, "a_s")
         h = {}
 
-        def scatter(first, tiles):
-            start = min(first, HALF)
-            for t in tiles:
-                nc.vector.tensor_tensor(
-                    page[t][:].indirect(list_slice(lists["offs2"], first, CHUNK)),
-                    h[first, t // 2][:, t % 2, :],
-                    gain[start][:, t, first - start : first - start + CHUNK],
-                    ALU.mult,
+        def product_b(out, t, first, count):
+            half, c0 = divmod(first, HALF)
+            for a in range(PASSES):
+                nc.tensor.matmul_mx(
+                    out=out,
+                    lhsT=w1_c[:, a, slot(t)].bitcast(FP8X4),
+                    lhsT_scale=w1_s[:, a, slot(t)],
+                    rhs=v_c[a, half][:, c0 : c0 + count].bitcast(FP8X4),
+                    rhs_scale=v_s[:, a, first : first + count],
+                    start=(a == 0), stop=(a == PASSES - 1),
                 )
 
-        for c in range(S // CHUNK):
+        def leading_a():
+            a_c = held([P, CHUNK], U32, "a_c0")
+            woven = []
+            for n0 in range(0, CHUNK, P):
+                acc = bank(BANKS_B[0], "acc_b")
+                for t in range(SLOTS):
+                    product_b(acc[:, slot(t)], t, n0, P)
+                gel = gelu_tile(P)
+                nc.scalar.activation(
+                    gel[:].rearrange("p t n -> p (t n)"), acc[:], ACT.Gelu_apprx_tanh
+                )
+                a_b = ring.tile([P, P, SLOTS], BF16, name="a_b", align_bytes=64)
+                nc.vector.tensor_tensor(
+                    weave_out(a_b[:]), weave_in(gel[:]),
+                    gm2[:].unsqueeze(1).unsqueeze(3).to_broadcast([P, P // 4, SLOTS, 4]),
+                    ALU.mult,
+                )
+                woven.append((n0, a_b))
+            for n0, a_b in woven:
+                nc.vector.quantize_mx(
+                    out=a_c[:, n0 : n0 + P].bitcast(FP8X4), scales=a_s[:, n0 : n0 + P],
+                    in_=a_b[:].rearrange("p n t -> p (n t)"),
+                )
+            return a_c
+
+        def later_a(c):
             first = c * CHUNK
-            u, c0 = divmod(first, HALF)
-            cols = slice(first, first + CHUNK)
-            if c == 0:
-                second_reading(first)
-            gel = ring.tile([P, PACK, CHUNK], F32, name="gel", tag="gel", align_bytes=64)
+            gel = gelu_tile(CHUNK)
             for pair in range(2):
-                acc = bank(("pb", "pa", "pb", "pc")[c], "acc1")
+                acc = bank(BANKS_B[c], "acc_b")
                 for s in range(2):
-                    t = 2 * pair + s
-                    for a in range(2):
-                        nc.tensor.matmul_mx(
-                            out=acc[:, s * CHUNK : (s + 1) * CHUNK],
-                            lhsT=w1_c[:, a, t * P : (t + 1) * P].bitcast(FP8X4),
-                            lhsT_scale=w1_s[:, a, t * P : (t + 1) * P],
-                            rhs=v_words[a][u][:, c0 : c0 + CHUNK].bitcast(FP8X4),
-                            rhs_scale=v_scale[:, a, cols],
-                            start=(a == 0), stop=(a == 1),
-                        )
+                    product_b(acc[:, s * CHUNK : (s + 1) * CHUNK], 2 * pair + s, first, CHUNK)
                 nc.scalar.activation(
                     gel[:, 2 * pair : 2 * pair + 2, :].rearrange("p s n -> p (s n)"),
                     acc[:], ACT.Gelu_apprx_tanh,
                 )
-            if c == 0:
-                pick_table(0, 1)
-                pick_table(1, 1)
-            a_b = ring.tile([P, CHUNK, PACK], BF16, name="a_b", align_bytes=64)
-            if c == 0:
-                nc.vector.tensor_tensor(
-                    weave_out(a_b[:]), weave_in(gel[:]),
-                    gm2[:].unsqueeze(1).unsqueeze(3).to_broadcast([P, CHUNK // 4, PACK, 4]),
-                    ALU.mult,
+            a_b = ring.tile([P, CHUNK, SLOTS], BF16, name="a_b", align_bytes=64)
+            a_rows = held([P, SLOTS, CHUNK], BF16, "a_rows")
+            for t in range(SLOTS):
+                nc.scalar.activation(
+                    a_rows[:, t, :], gel[:, t, :], ACT.Copy, scale=gm2[:, t : t + 1]
                 )
-            else:
-                a_rows = held([P, PACK, CHUNK], BF16, "a_rows")
-                for t in range(PACK):
-                    nc.scalar.activation(
-                        a_rows[:, t, :], gel[:, t, :], ACT.Copy, scale=gm2[:, t : t + 1]
-                    )
-                nc.scalar.copy(weave_out(a_b[:]), weave_in(a_rows[:]))
-            if c == 0:
-                a_c = held([P, CHUNK], U32, "a_c")
-            else:
-                a_c = slide.tile([P, CHUNK], U32, name="a_c%d" % c, offset=(c - 1) * KB, align_bytes=64)
+            nc.scalar.copy(weave_out(a_b[:]), weave_in(a_rows[:]))
+            a_c = placed([P, CHUNK], U32, "a_c%d" % c, H_AT[c - 1])
             nc.vector.quantize_mx(
-                out=a_c[:].bitcast(FP8X4), scales=a_s[:, cols],
+                out=a_c[:].bitcast(FP8X4), scales=a_s[:, first : first + CHUNK],
                 in_=a_b[:].rearrange("p n t -> p (n t)"),
             )
-            if c > 0:
-                second_reading(first)
-                scatter(first - CHUNK, (2, 3))
+            return a_c
+
+        def lower_reading(c, a_c, width):
+            first = c * CHUNK
             for pair in range(2):
-                acc = bank(("pd", "pc", "pd", "pc")[c], "acc2")
+                acc = bank(BANKS_FIRST[c], "acc_first")
                 for s in range(2):
-                    t = 2 * pair + s
-                    nc.tensor.matmul_mx(
-                        out=acc[:, s * CHUNK : (s + 1) * CHUNK],
-                        lhsT=w2_c[:, t * P : (t + 1) * P].bitcast(FP8X4),
-                        lhsT_scale=w2_s[:, t * P : (t + 1) * P],
-                        rhs=a_c[:].bitcast(FP8X4),
-                        rhs_scale=a_s[:, cols],
-                        start=True, stop=True,
-                    )
-                tile = slide.tile(
-                    [P, 2, CHUNK], F32, name="h%d%d" % (c, pair), offset=(c + 2 * pair) * KB,
-                    align_bytes=64,
+                    for n0 in range(0, CHUNK, width):
+                        nc.tensor.matmul_mx(
+                            out=acc[:, s * CHUNK + n0 : s * CHUNK + n0 + width],
+                            lhsT=w2_c[:, slot(2 * pair + s)].bitcast(FP8X4),
+                            lhsT_scale=w2_s[:, slot(2 * pair + s)],
+                            rhs=a_c[:, n0 : n0 + width].bitcast(FP8X4),
+                            rhs_scale=a_s[:, first + n0 : first + n0 + width],
+                            start=True, stop=True,
+                        )
+                h[c, pair] = placed(
+                    [P, 2, CHUNK], F32, "h%d%d" % (c, pair), H_AT[c] + 2 * pair * KB
                 )
-                h[first, pair] = tile
                 nc.vector.tensor_tensor(
-                    tile[:],
+                    h[c, pair][:],
                     acc[:].rearrange("p (s n) -> p s n", s=2),
-                    h3[:, 2 * pair : 2 * pair + 2, cols],
+                    second[:, 2 * pair : 2 * pair + 2, first : first + CHUNK],
                     ALU.min,
                 )
-            if c < S // CHUNK - 1:
-                scatter(first, (0, 1))
 
-        w4_b = held([P, PACK, P, PACK], BF16, "w4_b", tag="a_rows")
+        def scatter(c, slots):
+            first = c * CHUNK
+            loaded = min(first, HALF)
+            for t in slots:
+                nc.vector.tensor_tensor(
+                    page[t][:].indirect(list_slice(lists["offs2"], first, CHUNK)),
+                    h[c, t // 2][:, t % 2, :],
+                    gain[loaded][:, t, first - loaded : first - loaded + CHUNK],
+                    ALU.mult,
+                )
+
+        second_reading(0)
+        a_c = leading_a()
+        pick_words(1)
+        lower_reading(0, a_c, P)
+        for c in range(1, CHUNKS):
+            scatter(c - 1, (0, 1))
+            a_c = later_a(c)
+            second_reading(c)
+            scatter(c - 1, (2, 3))
+            lower_reading(c, a_c, CHUNK)
+
+        w4_b = held([P, SLOTS, P, SLOTS], BF16, "w4_b", after="a_rows")
         nc.scalar.copy(
             w4_b[:].rearrange("p t q j -> p q j t"),
-            w4_raw[:].rearrange("p j (q t) -> p q j t", t=PACK),
+            w4_raw[:].rearrange("p j (q t) -> p q j t", t=SLOTS),
         )
-        gg_neg = held([P, PACK], F32, "gg_neg")
+        gg_neg = held([P, SLOTS], F32, "gg_neg")
         nc.scalar.activation(gg_neg[:], gg_col[:], ACT.Copy, scale=-1.0)
-        w4_c = slide.tile([P, H], U32, name="w4_c", offset=3 * KB, align_bytes=64)
+        w4_c = placed([P, H], U32, "w4_c", H_AT[CHUNKS - 1])
         w4_s = held([P, H], U8, "w4_s")
         nc.vector.quantize_mx(
             out=w4_c[:].bitcast(FP8X4), scales=w4_s[:],
             in_=w4_b[:].rearrange("p t q j -> p (t q j)"),
         )
 
-        x_rows = [held([P, PACK, HALF], BF16, "x_rows%d" % u, tag="w1_raw%d" % u) for u in range(2)]
+        x_rows = [held([P, SLOTS, HALF], BF16, "x_rows%d" % half) for half in range(2)]
 
-        def reread(t):
-            pieces = 2 if t == PACK - 1 else 1
-            width = NP // pieces
+        def reread(t, width):
             picked = held([P, NP], F32, "picked%d" % t)
-            for piece in range(pieces):
-                cols = slice(piece * width, (piece + 1) * width)
+            for first in range(0, NP, width):
                 nc.vector.tensor_copy(
-                    picked[:, cols],
-                    page[t][:].indirect(list_slice(lists["offs3"], piece * width, width)),
+                    picked[:, first : first + width],
+                    page[t][:].indirect(list_slice(lists["offs3"], first, width)),
                 )
                 sine = held([P, width], F32, "sine")
-                nc.scalar.activation(sine[:], picked[:, cols], ACT.Sin, scale=gs_col[:, t : t + 1])
-                for u in range(2) if pieces == 1 else [piece]:
-                    c0 = u * HALF - piece * width
+                nc.scalar.activation(
+                    sine[:], picked[:, first : first + width], ACT.Sin, scale=gs_col[:, t : t + 1]
+                )
+                for c0 in range(0, width, HALF):
                     nc.scalar.activation(
-                        x_rows[u][:, t, :], sine[:, c0 : c0 + HALF], ACT.Copy,
+                        x_rows[(first + c0) // HALF][:, t, :], sine[:, c0 : c0 + HALF], ACT.Copy,
                         scale=gx_col[:, t : t + 1],
                     )
 
-        for t in range(PACK):
-            scatter(S - CHUNK, [t])
+        for t in range(SLOTS):
+            scatter(CHUNKS - 1, (t,))
             if t > 0:
-                reread(t - 1)
-        reread(PACK - 1)
+                reread(t - 1, NP)
+        reread(SLOTS - 1, HALF)
 
         x_c = held([P, NP], U32, "x_c")
         x_s = held([P, NP], U8, "x_s")
-        y = held([P, PACK, NP], F32, "y", tag="h3")
-        y_b = []
+        y = held([P, SLOTS, NP], F32, "y", after="w1_raw1")
         y_s = held([P, NP], U8, "y_s")
-        out_rows = out_0.rearrange("(p t) j -> t p j", t=PACK)
+        y_b = []
+        out_rows = out_0.rearrange("(p t) j -> t p j", t=SLOTS)
         out_words = out_1[0].rearrange("p m t -> p (m t)").bitcast(I32)
-        for u in range(2):
-            cols = slice(u * HALF, (u + 1) * HALF)
-            x_b = held([P, HALF, PACK], BF16, "x_b%d" % u, tag="x_b%d" % u)
-            nc.scalar.copy(weave_out(x_b[:]), weave_in(x_rows[u][:]))
-            if u == 0:
-                whole = held([P, PACK, HALF], F32, "golden0", tag="gain2")
-                golden = [whole[:, t, :] for t in range(PACK)]
-            else:
-                early = held([P, 2, HALF], F32, "golden1a")
-                late = held([P, 1, HALF], F32, "golden1b", tag="x_b0")
-                last = held([P, HALF], F32, "golden1c", tag="x_b1")
-                golden = [early[:, t, :] for t in range(2)] + [late[:, t, :] for t in range(1)] + [last[:]]
+
+        def golden_tiles(half):
+            if half == 0:
+                whole = held([P, SLOTS, HALF], F32, "golden0", after="gain2")
+                return [whole[:, t, :] for t in range(SLOTS)]
+            early = held([P, 2, HALF], F32, "golden1a")
+            late = held([P, 1, HALF], F32, "golden1b", after="x_rows0")
+            last = held([P, HALF], F32, "golden1c", after="x_rows1")
+            return [early[:, 0, :], early[:, 1, :], late[:, 0, :], last[:]]
+
+        for half in range(2):
+            cols = slice(half * HALF, (half + 1) * HALF)
+            x_b = held([P, HALF, SLOTS], BF16, "x_b%d" % half)
+            nc.scalar.copy(weave_out(x_b[:]), weave_in(x_rows[half][:]))
+            golden = golden_tiles(half)
             nc.vector.quantize_mx(
                 out=x_c[:, cols].bitcast(FP8X4), scales=x_s[:, cols],
                 in_=x_b[:].rearrange("p n t -> p (n t)"),
             )
-            for t in range(PACK):
+            for t in range(SLOTS):
                 nc.vector.tensor_copy(
-                    golden[t],
-                    page[t][:].indirect(list_slice(lists["offs4"], u * HALF, HALF)),
+                    golden[t], page[t][:].indirect(list_slice(lists["offs4"], half * HALF, HALF))
                 )
-            for t in range(PACK):
-                acc = bank(("pa", "pb")[t % 2], "acc4")
+            for t in range(SLOTS):
+                acc = bank("AB"[t % 2], "acc_y")
                 nc.tensor.matmul_mx(
                     out=acc[:],
-                    lhsT=w4_c[:, t * P : (t + 1) * P].bitcast(FP8X4),
-                    lhsT_scale=w4_s[:, t * P : (t + 1) * P],
+                    lhsT=w4_c[:, slot(t)].bitcast(FP8X4),
+                    lhsT_scale=w4_s[:, slot(t)],
                     rhs=x_c[:, cols].bitcast(FP8X4),
                     rhs_scale=x_s[:, cols],
                     start=True, stop=True,
                 )
                 nc.vector.scalar_tensor_tensor(
-                    y[:, t, cols], golden[t], gg_neg[:, t : t + 1], acc[:],
-                    ALU.mult, ALU.add,
+                    y[:, t, cols], golden[t], gg_neg[:, t : t + 1], acc[:], ALU.mult, ALU.add
                 )
                 nc.sync.dma_start(out_rows[t][:, cols], y[:, t, cols])
-            y_b.append(held([P, HALF, PACK], BF16, "y_b%d" % u, tag="w1_b%d" % u))
-            if u == 0:
-                nc.scalar.copy(weave_out(y_b[u][:]), weave_in(y[:, :, cols]))
-        split = 192
-        nc.scalar.copy(weave_out(y_b[1][:, 0:split, :]), weave_in(y[:, :, HALF : HALF + split]))
-        for u in range(2):
-            cols = slice(u * HALF, (u + 1) * HALF)
-            if u == 1:
-                nc.vector.tensor_copy(
-                    weave_out(y_b[1][:, split:HALF, :]), weave_in(y[:, :, HALF + split : NP])
-                )
-            y_c = held([P, HALF], I32, "y_c%d" % u, tag="x_b1" if u == 0 else None)
+            y_b.append(held([P, HALF, SLOTS], BF16, "y_b%d" % half, after="w1_b%d" % half))
+            on_scalar = HALF if half == 0 else Y_ON_SCALAR
+            nc.scalar.copy(
+                weave_out(y_b[half][:, 0:on_scalar, :]),
+                weave_in(y[:, :, half * HALF : half * HALF + on_scalar]),
+            )
+
+        def planes(half, y_c):
+            cols = slice(half * HALF, (half + 1) * HALF)
             nc.vector.quantize_mx(
                 out=y_c[:].bitcast(FP8X4), scales=y_s[:, cols],
-                in_=y_b[u][:].rearrange("p n t -> p (n t)"),
+                in_=y_b[half][:].rearrange("p n t -> p (n t)"),
             )
             nc.sync.dma_start(out_words[:, cols], y_c[:])
+
+        planes(0, held([P, HALF], I32, "y_c0", after="x_rows0"))
+        nc.vector.tensor_copy(
+            weave_out(y_b[1][:, Y_ON_SCALAR:HALF, :]), weave_in(y[:, :, HALF + Y_ON_SCALAR : NP])
+        )
+        planes(1, held([P, HALF], I32, "y_c1"))
         for q in range(4):
-            (nc.scalar if q % 2 == 0 else nc.sync).dma_start(
+            (nc.scalar, nc.sync)[q % 2].dma_start(
                 out_2[0, 4 * q : 4 * q + 4, :].bitcast(I32),
-                y_s[32 * q : 32 * q + 4, :].bitcast(I32),
+                y_s[QUADRANT * q : QUADRANT * q + 4, :].bitcast(I32),
             )

@@ -26,13 +26,13 @@ CHUNKS = S // CHUNK
 LIST_ROWS = 16
 KB = 1024
 
-W1_ON_SCALAR = 40
-Y_ON_SCALAR = 192
+W1_ON_SCALAR = 32
+Y_ON_SCALAR = 208
 
 H_AT = (0, KB, 5 * KB, 9 * KB)
 
 BANKS_B = "BABC"
-BANKS_SECOND = "ADDC"
+BANKS_SECOND = "ACDC"
 BANKS_FIRST = "DCDC"
 
 
@@ -46,6 +46,10 @@ def weave_out(tile):
 
 def weave_in(tile):
     return tile.rearrange("p t (c i) -> p c t i", i=4)
+
+
+def by_column(tile):
+    return tile.rearrange("p t n -> p n t")
 
 
 def slot(t):
@@ -301,7 +305,7 @@ def tile_list_panel_node_features_kernel(
                 nc.scalar.activation(
                     a_rows[:, t, :], gel[:, t, :], ACT.Copy, scale=gm2[:, t : t + 1]
                 )
-            nc.scalar.copy(weave_out(a_b[:]), weave_in(a_rows[:]))
+            nc.scalar.copy(a_b[:], by_column(a_rows[:]))
             a_c = placed([P, CHUNK], U32, "a_c%d" % c, H_AT[c - 1])
             nc.vector.quantize_mx(
                 out=a_c[:].bitcast(FP8X4), scales=a_s[:, first : first + CHUNK],
@@ -414,7 +418,7 @@ def tile_list_panel_node_features_kernel(
         for half in range(2):
             cols = slice(half * HALF, (half + 1) * HALF)
             x_b = held([P, HALF, SLOTS], BF16, "x_b%d" % half)
-            nc.scalar.copy(weave_out(x_b[:]), weave_in(x_rows[half][:]))
+            nc.scalar.copy(x_b[:], by_column(x_rows[half][:]))
             golden = golden_tiles(half)
             nc.vector.quantize_mx(
                 out=x_c[:, cols].bitcast(FP8X4), scales=x_s[:, cols],
@@ -441,8 +445,8 @@ def tile_list_panel_node_features_kernel(
             y_b.append(held([P, HALF, SLOTS], BF16, "y_b%d" % half, after="w1_b%d" % half))
             on_scalar = HALF if half == 0 else Y_ON_SCALAR
             nc.scalar.copy(
-                weave_out(y_b[half][:, 0:on_scalar, :]),
-                weave_in(y[:, :, half * HALF : half * HALF + on_scalar]),
+                y_b[half][:, 0:on_scalar, :],
+                by_column(y[:, :, half * HALF : half * HALF + on_scalar]),
             )
 
         def planes(half, y_c):

from contextlib import ExitStack

import concourse.mybir as mybir

K, M, H, T, S, T2, NP = 1024, 512, 512, 4096, 1024, 2048, 1024
FLOPS = 2 * (K * M * S + M * H * S + K * H * S + H * H * NP)

F32 = mybir.dt.float32
BF16 = mybir.dt.bfloat16
I32 = mybir.dt.int32
U32 = mybir.dt.uint32
U16 = mybir.dt.uint16
U8 = mybir.dt.uint8
FP8X4 = mybir.dt.float8_e4m3fn_x4
FP4X4 = mybir.dt.float4_e2m1fn_x4
ALU = mybir.AluOpType
ACT = mybir.ActivationFunctionType

P = 128
SLOTS = 4
PASSES = K // (P * SLOTS)
QUADRANT = 32
HALF = 512
CHUNK = 256
CHUNKS = S // CHUNK
LIST_ROWS = 16
KB = 1024

W1_ON_SCALAR = 32
Y_ON_SCALAR = 208

H_AT = (0, KB, 5 * KB, 9 * KB)

BANKS_B = "BABC"
BANKS_SECOND = "ACDC"
BANKS_FIRST = "DCDC"


def list_slice(offsets, first, count):
    return offsets[:, first // LIST_ROWS : (first + count) // LIST_ROWS]


def weave_out(tile):
    return tile.rearrange("p (c i) t -> p c t i", i=4)


def weave_in(tile):
    return tile.rearrange("p t (c i) -> p c t i", i=4)


def by_column(tile):
    return tile.rearrange("p t n -> p n t")


def slot(t):
    return slice(t * P, (t + 1) * P)


def tile_list_panel_node_features_kernel(
    tc, tab_words, tab_scales, offs, w1, gm, w2_words, w2_scales, w3_words, w3_scales,
    wgs, page0, offs2, offs3, gs, gx, w4, offs4, gg, out_0, out_1, out_2,
):
    nc = tc.nc
    with ExitStack() as ctx:
        keep = ctx.enter_context(tc.tile_pool(name="keep", bufs=1))
        staged = ctx.enter_context(tc.tile_pool(name="staged", bufs=1))
        ring = ctx.enter_context(tc.tile_pool(name="ring", bufs=2))
        psum = ctx.enter_context(tc.psum_pool(name="psum", bufs=1))

        def held(shape, dtype, name, after=None):
            return keep.tile(shape, dtype, name=name, tag=after or name, align_bytes=64)

        def placed(shape, dtype, name, offset):
            return staged.tile(shape, dtype, name=name, offset=offset, align_bytes=64)

        def bank(pair, name):
            return psum.tile([P, HALF], F32, name=name, tag=pair, bufs=2)

        def gelu_tile(columns):
            return ring.tile([P, SLOTS, columns], F32, name="gel", align_bytes=64)

        lists = {}
        for name in ("offs", "offs2", "offs3", "offs4"):
            lists[name] = held([P, S // LIST_ROWS], U16, "list_" + name)

        tab_s = held([P, T], U8, "tab_s")
        w_s_raw = held([P, PASSES + 1, H], U8, "w_s_raw")
        v_s = held([P, PASSES, S], U8, "v_s")
        warm = held([P, 1], F32, "warm")
        nc.vector.memset(w_s_raw[:].rearrange("p a c -> p (a c)").bitcast(I32), 0)
        nc.vector.memset(tab_s[32:64, :].bitcast(I32), 0)
        nc.vector.memset(tab_s[64:128, :].bitcast(I32), 0)
        nc.vector.memset(v_s[:].rearrange("p a c -> p (a c)").bitcast(I32), 0)

        nc.sync.dma_start(
            tab_s[0:32, :].bitcast(I32), tab_scales.rearrange("a q t -> (a q) t").bitcast(I32)
        )
        nc.sync.dma_start(lists["offs"][:], offs)
        w3_raw = held([P, PASSES, 2 * H], U8, "w3_raw")
        nc.sync.dma_start(w3_raw[:].bitcast(I32), w3_words.rearrange("a p b -> p a b").bitcast(I32))
        for q in range(4):
            nc.scalar.dma_start(
                w_s_raw[QUADRANT * q : QUADRANT * q + 4, 0:PASSES, :].bitcast(I32),
                w3_scales[:, 4 * q : 4 * q + 4, :].rearrange("a r c -> r a c").bitcast(I32),
            )
        nc.vector.memset(warm[:], 0.0)
        warm_out = held([P, 1], F32, "warm_out")
        nc.scalar.activation(warm_out[:], warm[:], ACT.Gelu_apprx_tanh)

        picked_s = held([P, S], U8, "picked_s")
        nc.vector.tensor_copy(picked_s[:], tab_s[:].indirect(lists["offs"][:]))

        def move_scale_rows(a, queue):
            for q in range(4):
                row = 16 * a + 4 * q
                queue.dma_start(
                    v_s[QUADRANT * q : QUADRANT * q + 4, a, :].bitcast(I32),
                    picked_s[row : row + 4, :].bitcast(I32),
                )

        tab_rows = tab_words.rearrange("a p t i -> a p (t i)").bitcast(I32)
        w1_rows = w1.rearrange("(a p j) m -> a p j m", a=PASSES, j=SLOTS)
        tab_w = [held([P, T], I32, "tab_w%d" % a) for a in range(PASSES)]
        w1_raw = [held([P, SLOTS, M], F32, "w1_raw%d" % a) for a in range(PASSES)]
        nc.sync.dma_start(tab_w[0][:], tab_rows[0])
        nc.sync.dma_start(w1_raw[0][:], w1_rows[0])
        nc.sync.dma_start(tab_w[1][:], tab_rows[1])
        move_scale_rows(0, nc.sync)
        nc.sync.dma_start(w1_raw[1][:], w1_rows[1])
        move_scale_rows(1, nc.gpsimd)

        w3_c = held([P, PASSES, 2 * H], U8, "w3_c")
        nc.vector.tensor_copy(
            w3_c[:].bitcast(U16).rearrange("p a (t q) -> p a q t", t=SLOTS),
            w3_raw[:].bitcast(U16).rearrange("p a (q t) -> p a q t", t=SLOTS),
        )

        v_c = {}

        def pick_words(half):
            for a in range(PASSES):
                words = held([P, HALF], I32, "v_c%d%d" % (a, half))
                nc.vector.tensor_copy(
                    words[:].bitcast(U32),
                    tab_w[a][:].bitcast(U32).indirect(list_slice(lists["offs"], half * HALF, HALF)),
                )
                v_c[a, half] = words

        pick_words(0)

        w1_c = held([P, PASSES, M], U32, "w1_c")
        w1_s = held([P, PASSES, M], U8, "w1_s")
        w1_b = [held([P, SLOTS, P, SLOTS], BF16, "w1_b%d" % a) for a in range(PASSES)]
        shares = ((nc.scalar.copy, 0, W1_ON_SCALAR), (nc.vector.tensor_copy, W1_ON_SCALAR, P))
        for a in range(PASSES):
            for copy, q0, q1 in shares:
                copy(
                    w1_b[a][:, :, q0:q1, :].rearrange("p t q j -> p q j t"),
                    w1_raw[a][:, :, SLOTS * q0 : SLOTS * q1].rearrange("p j (q t) -> p q j t", t=SLOTS),
                )
            nc.vector.quantize_mx(
                out=w1_c[:, a, :].bitcast(FP8X4), scales=w1_s[:, a, :],
                in_=w1_b[a][:].rearrange("p t q j -> p (t q j)"),
            )
        w3_s = held([P, PASSES, H], U8, "w3_s")
        nc.vector.tensor_copy(
            w3_s[:].rearrange("p a (t q) -> p a q t", t=SLOTS),
            w_s_raw[:, 0:PASSES, :].rearrange("p a (q t) -> p a q t", t=SLOTS),
        )

        second = held([P, SLOTS, S], F32, "second", after="w1_raw1")

        def second_reading(c):
            first = c * CHUNK
            half, c0 = divmod(first, HALF)
            for pair in range(2):
                acc = bank(BANKS_SECOND[c], "acc_second")
                for s in range(2):
                    t = 2 * pair + s
                    for n0 in range(0, CHUNK, P):
                        for a in range(PASSES):
                            nc.tensor.matmul_mx(
                                out=acc[:, s * CHUNK + n0 : s * CHUNK + n0 + P],
                                lhsT=w3_c[:, a, 2 * t * P : 2 * (t + 1) * P].bitcast(FP4X4),
                                lhsT_scale=w3_s[:, a, slot(t)],
                                rhs=v_c[a, half][:, c0 + n0 : c0 + n0 + P].bitcast(FP8X4),
                                rhs_scale=v_s[:, a, first + n0 : first + n0 + P],
                                start=(a == 0), stop=(a == PASSES - 1),
                            )
                nc.scalar.copy(
                    second[:, 2 * pair : 2 * pair + 2, first : first + CHUNK],
                    acc[:].rearrange("p (s n) -> p s n", s=2),
                )

        w2_raw = held([P, H], I32, "w2_raw")
        nc.sync.dma_start(w2_raw[:], w2_words[0].rearrange("p c i -> p (c i)").bitcast(I32))
        for q in range(4):
            nc.sync.dma_start(
                w_s_raw[QUADRANT * q : QUADRANT * q + 4, PASSES, :].bitcast(I32),
                w2_scales[0, 4 * q : 4 * q + 4, :].bitcast(I32),
            )
        gm_col = held([P, SLOTS], F32, "gm_col")
        nc.sync.dma_start(gm_col[:], gm.rearrange("(p t) -> p t", t=SLOTS))
        gm2 = held([P, SLOTS], F32, "gm2")
        nc.vector.tensor_scalar(gm2[:], gm_col[:], 2.0, None, ALU.mult)

        page_rows = page0.rearrange("(p t) c -> t p c", t=SLOTS)
        wgs_rows = wgs.rearrange("(i t) j -> i t j", t=SLOTS)
        page = [held([P, T2], F32, "page%d" % t) for t in range(SLOTS)]
        gain = {
            0: held([P, SLOTS, CHUNK], F32, "gain0"),
            CHUNK: held([P, SLOTS, CHUNK], F32, "gain1"),
            HALF: held([P, SLOTS, HALF], F32, "gain2"),
        }

        def load_gain(first, count):
            for q in (0, 2, 1, 3):
                nc.sync.dma_start(
                    gain[first][QUADRANT * q : QUADRANT * (q + 1), :, :],
                    wgs_rows[:, :, first : first + count],
                )

        nc.sync.dma_start(page[0][:], page_rows[0])
        nc.sync.dma_start(lists["offs2"][:], offs2)
        load_gain(0, CHUNK)
        for t in range(1, SLOTS):
            nc.sync.dma_start(page[t][:], page_rows[t])
        load_gain(CHUNK, CHUNK)
        w4_raw = held([P, SLOTS, H], F32, "w4_raw")
        nc.sync.dma_start(w4_raw[:], w4.rearrange("(p j) n -> p j n", j=SLOTS))
        load_gain(HALF, HALF)
        nc.sync.dma_start(lists["offs3"][:], offs3)
        nc.sync.dma_start(lists["offs4"][:], offs4)
        gs_col = held([P, SLOTS], F32, "gs_col")
        gx_col = held([P, SLOTS], F32, "gx_col")
        gg_col = held([P, SLOTS], F32, "gg_col")
        for column, vec in ((gs_col, gs), (gx_col, gx), (gg_col, gg)):
            nc.sync.dma_start(column[:], vec.rearrange("(p t) -> p t", t=SLOTS))

        w2_c = held([P, H], I32, "w2_c", after="w1_b1")
        w2_s = held([P, H], U8, "w2_s")
        nc.vector.tensor_copy(
            w2_c[:].rearrange("p (t q) -> p q t", t=SLOTS),
            w2_raw[:].rearrange("p (q t) -> p q t", t=SLOTS),
        )
        nc.vector.tensor_copy(
            w2_s[:].rearrange("p (t q) -> p q t", t=SLOTS),
            w_s_raw[:, PASSES, :].rearrange("p (q t) -> p q t", t=SLOTS),
        )

        a_s = held([P, S], U8, "a_s")
        h = {}

        def product_b(out, t, first, count):
            half, c0 = divmod(first, HALF)
            for a in range(PASSES):
                nc.tensor.matmul_mx(
                    out=out,
                    lhsT=w1_c[:, a, slot(t)].bitcast(FP8X4),
                    lhsT_scale=w1_s[:, a, slot(t)],
                    rhs=v_c[a, half][:, c0 : c0 + count].bitcast(FP8X4),
                    rhs_scale=v_s[:, a, first : first + count],
                    start=(a == 0), stop=(a == PASSES - 1),
                )

        def leading_a():
            a_c = held([P, CHUNK], U32, "a_c0")
            woven = []
            for n0 in range(0, CHUNK, P):
                acc = bank(BANKS_B[0], "acc_b")
                for t in range(SLOTS):
                    product_b(acc[:, slot(t)], t, n0, P)
                gel = gelu_tile(P)
                nc.scalar.activation(
                    gel[:].rearrange("p t n -> p (t n)"), acc[:], ACT.Gelu_apprx_tanh
                )
                a_b = ring.tile([P, P, SLOTS], BF16, name="a_b", align_bytes=64)
                nc.vector.tensor_tensor(
                    weave_out(a_b[:]), weave_in(gel[:]),
                    gm2[:].unsqueeze(1).unsqueeze(3).to_broadcast([P, P // 4, SLOTS, 4]),
                    ALU.mult,
                )
                woven.append((n0, a_b))
            for n0, a_b in woven:
                nc.vector.quantize_mx(
                    out=a_c[:, n0 : n0 + P].bitcast(FP8X4), scales=a_s[:, n0 : n0 + P],
                    in_=a_b[:].rearrange("p n t -> p (n t)"),
                )
            return a_c

        def later_a(c):
            first = c * CHUNK
            gel = gelu_tile(CHUNK)
            for pair in range(2):
                acc = bank(BANKS_B[c], "acc_b")
                for s in range(2):
                    product_b(acc[:, s * CHUNK : (s + 1) * CHUNK], 2 * pair + s, first, CHUNK)
                nc.scalar.activation(
                    gel[:, 2 * pair : 2 * pair + 2, :].rearrange("p s n -> p (s n)"),
                    acc[:], ACT.Gelu_apprx_tanh,
                )
            a_b = ring.tile([P, CHUNK, SLOTS], BF16, name="a_b", align_bytes=64)
            a_rows = held([P, SLOTS, CHUNK], BF16, "a_rows")
            for t in range(SLOTS):
                nc.scalar.activation(
                    a_rows[:, t, :], gel[:, t, :], ACT.Copy, scale=gm2[:, t : t + 1]
                )
            nc.scalar.copy(a_b[:], by_column(a_rows[:]))
            a_c = placed([P, CHUNK], U32, "a_c%d" % c, H_AT[c - 1])
            nc.vector.quantize_mx(
                out=a_c[:].bitcast(FP8X4), scales=a_s[:, first : first + CHUNK],
                in_=a_b[:].rearrange("p n t -> p (n t)"),
            )
            return a_c

        def lower_reading(c, a_c, width):
            first = c * CHUNK
            for pair in range(2):
                acc = bank(BANKS_FIRST[c], "acc_first")
                for s in range(2):
                    for n0 in range(0, CHUNK, width):
                        nc.tensor.matmul_mx(
                            out=acc[:, s * CHUNK + n0 : s * CHUNK + n0 + width],
                            lhsT=w2_c[:, slot(2 * pair + s)].bitcast(FP8X4),
                            lhsT_scale=w2_s[:, slot(2 * pair + s)],
                            rhs=a_c[:, n0 : n0 + width].bitcast(FP8X4),
                            rhs_scale=a_s[:, first + n0 : first + n0 + width],
                            start=True, stop=True,
                        )
                h[c, pair] = placed(
                    [P, 2, CHUNK], F32, "h%d%d" % (c, pair), H_AT[c] + 2 * pair * KB
                )
                nc.vector.tensor_tensor(
                    h[c, pair][:],
                    acc[:].rearrange("p (s n) -> p s n", s=2),
                    second[:, 2 * pair : 2 * pair + 2, first : first + CHUNK],
                    ALU.min,
                )

        def scatter(c, slots):
            first = c * CHUNK
            loaded = min(first, HALF)
            for t in slots:
                nc.vector.tensor_tensor(
                    page[t][:].indirect(list_slice(lists["offs2"], first, CHUNK)),
                    h[c, t // 2][:, t % 2, :],
                    gain[loaded][:, t, first - loaded : first - loaded + CHUNK],
                    ALU.mult,
                )

        second_reading(0)
        a_c = leading_a()
        pick_words(1)
        lower_reading(0, a_c, P)
        for c in range(1, CHUNKS):
            scatter(c - 1, (0, 1))
            a_c = later_a(c)
            second_reading(c)
            scatter(c - 1, (2, 3))
            lower_reading(c, a_c, CHUNK)

        w4_b = held([P, SLOTS, P, SLOTS], BF16, "w4_b", after="a_rows")
        nc.scalar.copy(
            w4_b[:].rearrange("p t q j -> p q j t"),
            w4_raw[:].rearrange("p j (q t) -> p q j t", t=SLOTS),
        )
        gg_neg = held([P, SLOTS], F32, "gg_neg")
        nc.scalar.activation(gg_neg[:], gg_col[:], ACT.Copy, scale=-1.0)
        w4_c = placed([P, H], U32, "w4_c", H_AT[CHUNKS - 1])
        w4_s = held([P, H], U8, "w4_s")
        nc.vector.quantize_mx(
            out=w4_c[:].bitcast(FP8X4), scales=w4_s[:],
            in_=w4_b[:].rearrange("p t q j -> p (t q j)"),
        )

        x_rows = [held([P, SLOTS, HALF], BF16, "x_rows%d" % half) for half in range(2)]

        def reread(t, width):
            picked = held([P, NP], F32, "picked%d" % t)
            for first in range(0, NP, width):
                nc.vector.tensor_copy(
                    picked[:, first : first + width],
                    page[t][:].indirect(list_slice(lists["offs3"], first, width)),
                )
                sine = held([P, width], F32, "sine")
                nc.scalar.activation(
                    sine[:], picked[:, first : first + width], ACT.Sin, scale=gs_col[:, t : t + 1]
                )
                for c0 in range(0, width, HALF):
                    nc.scalar.activation(
                        x_rows[(first + c0) // HALF][:, t, :], sine[:, c0 : c0 + HALF], ACT.Copy,
                        scale=gx_col[:, t : t + 1],
                    )

        for t in range(SLOTS):
            scatter(CHUNKS - 1, (t,))
            if t > 0:
                reread(t - 1, NP)
        reread(SLOTS - 1, HALF)

        x_c = held([P, NP], U32, "x_c")
        x_s = held([P, NP], U8, "x_s")
        y = held([P, SLOTS, NP], F32, "y", after="w1_raw1")
        y_s = held([P, NP], U8, "y_s")
        y_b = []
        out_rows = out_0.rearrange("(p t) j -> t p j", t=SLOTS)
        out_words = out_1[0].rearrange("p m t -> p (m t)").bitcast(I32)

        def golden_tiles(half):
            if half == 0:
                whole = held([P, SLOTS, HALF], F32, "golden0", after="gain2")
                return [whole[:, t, :] for t in range(SLOTS)]
            early = held([P, 2, HALF], F32, "golden1a")
            late = held([P, 1, HALF], F32, "golden1b", after="x_rows0")
            last = held([P, HALF], F32, "golden1c", after="x_rows1")
            return [early[:, 0, :], early[:, 1, :], late[:, 0, :], last[:]]

        for half in range(2):
            cols = slice(half * HALF, (half + 1) * HALF)
            x_b = held([P, HALF, SLOTS], BF16, "x_b%d" % half)
            nc.scalar.copy(x_b[:], by_column(x_rows[half][:]))
            golden = golden_tiles(half)
            nc.vector.quantize_mx(
                out=x_c[:, cols].bitcast(FP8X4), scales=x_s[:, cols],
                in_=x_b[:].rearrange("p n t -> p (n t)"),
            )
            for t in range(SLOTS):
                nc.vector.tensor_copy(
                    golden[t], page[t][:].indirect(list_slice(lists["offs4"], half * HALF, HALF))
                )
            for t in range(SLOTS):
                acc = bank("AB"[t % 2], "acc_y")
                nc.tensor.matmul_mx(
                    out=acc[:],
                    lhsT=w4_c[:, slot(t)].bitcast(FP8X4),
                    lhsT_scale=w4_s[:, slot(t)],
                    rhs=x_c[:, cols].bitcast(FP8X4),
                    rhs_scale=x_s[:, cols],
                    start=True, stop=True,
                )
                nc.vector.scalar_tensor_tensor(
                    y[:, t, cols], golden[t], gg_neg[:, t : t + 1], acc[:], ALU.mult, ALU.add
                )
                nc.sync.dma_start(out_rows[t][:, cols], y[:, t, cols])
            y_b.append(held([P, HALF, SLOTS], BF16, "y_b%d" % half, after="w1_b%d" % half))
            on_scalar = HALF if half == 0 else Y_ON_SCALAR
            nc.scalar.copy(
                y_b[half][:, 0:on_scalar, :],
                by_column(y[:, :, half * HALF : half * HALF + on_scalar]),
            )

        def planes(half, y_c):
            cols = slice(half * HALF, (half + 1) * HALF)
            nc.vector.quantize_mx(
                out=y_c[:].bitcast(FP8X4), scales=y_s[:, cols],
                in_=y_b[half][:].rearrange("p n t -> p (n t)"),
            )
            nc.sync.dma_start(out_words[:, cols], y_c[:])

        planes(0, held([P, HALF], I32, "y_c0", after="x_rows0"))
        nc.vector.tensor_copy(
            weave_out(y_b[1][:, Y_ON_SCALAR:HALF, :]), weave_in(y[:, :, HALF + Y_ON_SCALAR : NP])
        )
        planes(1, held([P, HALF], I32, "y_c1"))
        for q in range(4):
            (nc.scalar, nc.sync)[q % 2].dma_start(
                out_2[0, 4 * q : 4 * q + 4, :].bitcast(I32),
                y_s[QUADRANT * q : QUADRANT * q + 4, :].bitcast(I32),
            )
